import numpy as np, ml_dtypes
CORES = [10,34,74,98]
N = 4
import mx_ref
BF = ml_dtypes.bfloat16
def pick(q, e):
    c = np.concatenate([q[0].reshape(128, -1, 4), np.zeros((128, 1, 4), np.uint8)], axis=1); s = np.concatenate([q[1], np.ones((16, 1), np.uint8)], axis=1)
    return (np.ascontiguousarray(c[:, e].reshape(128, -1)), np.ascontiguousarray(s[:, e]))
def join(*qs):
    return (np.concatenate([q[0] for q in qs], axis=1), np.concatenate([q[1] for q in qs], axis=1))
def put(q, e, v):
    c, s = q[0].reshape(128, -1, 4).copy(), q[1].copy(); c[:, e] = v[0].reshape(128, -1, 4); s[:, e] = v[1]
    return (c.reshape(128, -1), s)
def pk(c, s):
    return (np.ascontiguousarray(c), mx_ref.live(s))
def emit(q):
    return q[0], q[1]
def decode(q):
    o = []
    for b in range(4):
        e = np.zeros((128, 128, 4), np.float32); e[np.arange(128), np.arange(128), b] = 1
        o.append(mx_ref.matmul(mx_ref.quantize(e.reshape(128, 512).astype(BF)), q))
    return np.stack(o, axis=2).reshape(128, -1)
def f(rng, *shape):
    return mx_ref.flush((rng.standard_normal(shape, dtype=np.float32) * np.exp2(rng.integers(-2, 3, shape[:-1] + (1,)))).astype(BF))
def wide(rng, *shape, cols=0):
    v = rng.standard_normal(shape, dtype=np.float32) * np.exp2(rng.integers(-12, 13, shape)).astype(np.float32)
    if cols: v *= np.repeat(np.exp2(rng.integers(-cols, cols + 1, shape[:-2] + (1, shape[-1] // 4))) * (rng.random(shape[:-2] + (1, shape[-1] // 4)) > 0.0625), 4, axis=-1).astype(np.float32)
    return mx_ref.flush(v.astype(BF))
P, CAP, M, S = 20, 12, 32, 48
def big(v):
    v = np.array(v, np.float32)
    v[np.abs(v) < np.float32(2.0 ** -16)] = 0
    return v.astype(BF)
def setup_inputs(rng):
    u = big(f(rng, N, 128, 512))
    u[:, :, 8:] = 0
    return {"r0": big(f(rng, N, 128, 4 * P)), "r1": big(f(rng, N, 128, 16 * P)), "r2": big(f(rng, N, 128, 64 * P)), "u": u, "w": f(rng, N, 128, 512)}
def setup_inputs_far(rng):
    d = setup_inputs(rng)
    low = rng.permutation(N) < N // 2
    i = np.arange(128)
    side = np.where(i < 48, -1, np.where(i < 80, 0, 1))
    o, c = rng.permutation(N), rng.permutation(N // 2 * P)[:M // 8]
    kind = np.full((N, P), -1)
    kind[o[:N // 2], rng.integers(0, P, N // 2)] = 0
    kind[o[N // 2 + c // P], c % P] = 1
    on = (side[None, :, None] == 0) | (side[None, :, None] == kind[:, None, :])
    for k, m in (("r0", on), ("r1", np.repeat(on | (kind != 0)[:, None, :], 4, axis=2))):
        v = (1.5 + 0.5 * rng.random((N, 128, m.shape[2], 4))) * 2.0 ** 26
        d[k] = big((v * m[:, :, :, None]).reshape(N, 128, -1))
    g = np.where(low[:, None], -1, side[None, :])
    d["u"][:, :, :4] = big((1.875 + 0.125 * rng.random((N, 128, 4))) * 2.0 ** 29 * g[:, :, None])
    h = d["u"][:, :, 4:8].astype(np.float32) * (side == 0)[None, :, None]
    d["u"][:, :, 4:8] = big(np.where(low[:, None, None], (1.875 + 0.125 * rng.random((N, 128, 4))) * 2.0 ** 26, h))
    return d
def setup_inputs_near(rng):
    d = setup_inputs(rng)
    t = N * np.arange(P)[None, :] + rng.permutation(N)[:, None]
    a, b, u = np.zeros((N, 128, P, 4), np.float32), np.zeros((N, 128, 4 * P, 4), np.float32), np.zeros((N, 128, 512), np.float32)
    a[:, :64] = rng.integers(4, 8, (64, 4))[None, :, None, :]
    for i in range(3): a[:, 64, :, i] = t // 8 ** i % 8
    b[:, 64, :, 3] = np.arange(4 * P) % 4
    a[:, 72:] = f(rng, N, 56, 4 * P).astype(np.float32).reshape(N, 56, P, 4)
    b[:, 72:] = f(rng, N, 56, 16 * P).astype(np.float32).reshape(N, 56, 4 * P, 4)
    u[:, :64, :4] = 1024 * rng.integers(4, 8, (N, 64, 4))
    u[:, 64, :4] = np.array([4, 32, 256, 1])[None, :] * (1 - 2 * (np.arange(N) % 2))[:, None]
    u[:, 72:, 4:8] = f(rng, N, 56, 4).astype(np.float32)
    return {**d, "r0": big(a.reshape(N, 128, -1)), "r1": big(b.reshape(N, 128, -1)), "u": big(u)}
def setup_inputs_pile(rng):
    d = setup_inputs(rng)
    of = np.arange(128) // (128 // N)
    a, b = np.zeros((N, N)), np.full((N, N), 4.0)
    for r in range(N):
        o = rng.permutation(N)
        o = o[o != r]
        o = np.concatenate([[r], o]) if r % 2 == 0 else np.concatenate([o, [r]])
        a[r, o] = 2.0 ** (10 - 2 * np.arange(N))
        b[r, o[(M - 1) // P]] = 2.0 ** 14
    d["r0"] = big((1 + rng.random((N, 128, 4 * P))) * a[of].T[:, :, None])
    d["r1"] = big((1 + rng.random((N, 128, 16 * P))) * b[of].T[:, :, None])
    d["u"][:, :, :4] = big((1 + rng.random((N, 128, 4))) * (of[None, :] == np.arange(N)[:, None])[:, :, None])
    return d
def setup_inputs_spread(rng):
    d = setup_inputs(rng)
    a = wide(rng, N, 128, 4 * P, cols=6).astype(np.float32).reshape(N, 128, P, 4)
    b = wide(rng, N, 128, 16 * P, cols=6).astype(np.float32).reshape(N, 128, 4 * P, 4)
    c = wide(rng, N, 128, 64 * P, cols=6).astype(np.float32).reshape(N, 128, 16 * P, 4)
    for q in range(N):
        n = rng.permutation(P)[:2]
        x = (1 + rng.random((128, 1, 4))) * 2.0 ** 26 * rng.choice([-1.0, 1.0], (128, 1, 4))
        a[q][:, n] = np.concatenate([x, -x], axis=1)
        b[q][:, 4 * n] = -a[q][:, n]
        b[q][:, 4 * n + 1] = 0
        c[q][:, 4 * (4 * n + 1)] = -a[q][:, n]
    return {**d, "r0": big(a.reshape(N, 128, -1)), "r1": big(b.reshape(N, 128, -1)), "r2": big(c.reshape(N, 128, -1))}
def setup_inputs_ties(rng):
    d = setup_inputs(rng)
    x = np.abs(big(f(rng, 128, 4)).astype(np.float32))
    a = np.ones((N, P), np.float32)
    for q in range(N): a[q, 1 + rng.permutation(P - 1)[:M // 2 // N]] = 2
    b = np.where(np.arange(4)[None, None, :] == rng.integers(0, 4, (N, P))[:, :, None], 3 - a[:, :, None], 0.125).reshape(N, 4 * P)
    d["r0"] = big((x[None, :, None, :] * a[:, None, :, None]).reshape(N, 128, -1))
    d["r1"] = big((x[None, :, None, :] * b[:, None, :, None]).reshape(N, 128, -1))
    d["u"][:, :, :4] = np.abs(d["u"][:, :, :4].astype(np.float32)).astype(BF)
    return d
def check_inputs(d):
    b = []
    def bad(v, lo, hi):
        v = np.abs(v.astype(np.float32))
        return not (np.isfinite(v).all() and ((v == 0) | (v >= lo) & (v <= hi)).all())
    for k in ("u", "w"):
        if bad(d[k], 2.0 ** -30, 2.0 ** 30): b.append("a value of " + k)
    for k in ("r0", "r1", "r2"):
        if bad(d[k], 2.0 ** -16, 2.0 ** 27): b.append("a value of " + k)
    if bad(d["u"][:, :, 4:8], 2.0 ** -16, 2.0 ** 27): b.append("a value of column 1 of u")
    if (d["u"][:, :, 8:].astype(np.float32) != 0).any(): b.append("u has numbers behind its first 2 columns")
    return b
def take(s, own):
    s = s + np.float32(0.0)
    at = np.flatnonzero(own >= 0)
    best = at[np.argsort(-s[at], kind="stable")][:M]
    got = np.full((N, CAP), -1)
    for q in range(N):
        k = best[own[best] == q][:CAP]
        got[q, :k.size] = k
    return got
def held(q, e):
    return decode(pick(q, np.concatenate([e, np.full(-len(e) % 4, -1)]))).reshape(128, -1, 4)[:, :len(e)]
def reference(r0, r1, r2, u, w):
    y, nm = np.zeros((N, 128, 2 * N * S), np.float32), np.full((N, 1, 2 * N * S), -1, np.float32)
    oc, osc = np.zeros((N, 128, 4 * N * S), np.uint8), np.zeros((N, 16, N * S), np.uint8)
    roots = join(*[mx_ref.quantize(np.ascontiguousarray(r0[q])) for q in range(N)])
    res = [join(*[mx_ref.quantize(np.ascontiguousarray(a[q])) for q in range(N)]) for a in (r1, r2)]
    to = np.arange(N * S) // S
    for r in range(N):
        uq, wq = mx_ref.quantize(np.ascontiguousarray(u[r])), mx_ref.quantize(np.ascontiguousarray(w[r]))
        shift = held(uq, np.arange(1, 2))[:, 0]
        pool, own, num = roots, np.repeat(np.arange(N), P), np.tile(np.arange(P), N)
        for t in range(2):
            parent = np.repeat(take(mx_ref.matmul(uq, pool)[0], own).reshape(-1), 4)
            on = np.flatnonzero(parent >= 0)
            new = np.full(N * S, -1)
            new[on] = 4 * num[parent[on]] + on % 4
            e, back = np.unique(parent[on], return_inverse=True)
            v = np.zeros((128, N * S, 4), np.float32)
            v[:, on] = (held(pool, e)[:, back] + held(res[t], 4 ** (t + 1) * P * to[on] + new[on])) + shift[:, None, :]
            pool, own, num = mx_ref.quantize(np.ascontiguousarray(v.reshape(128, -1).astype(BF))), np.where(parent >= 0, to, -1), new
            i = t * N * S
            y[r, :, i:i + N * S] = mx_ref.matmul(wq, pool)
            nm[r, 0, i:i + N * S] = num
        oc[r], osc[r] = emit(pool)
    return {"y": y, "oc": oc, "osc": osc, "nm": nm}

@@ -1,0 +1,382 @@
+from concourse.bass import DstId, RemoteDMATransfer
+from concourse.mybir import dt, AluOpType, AxisListType, ActivationFunctionType
+
+FP8 = "float8_e4m3fn_x4"
+SCRATCH = {}
+for _n, _w in (("P0", 188), ("P1", 368), ("R2", 322), ("W", 128), ("E", 512), ("UR", 128), ("V1", 128), ("E1", 128),
+               ("X1", 130), ("O1", 192), ("V2", 192), ("E2", 192), ("SN", 144), ("X2", 192)):
+    SCRATCH[_n + "c"] = ("sbuf", [128, _w], FP8)
+    SCRATCH[_n + "s"] = ("sbuf", [128, _w], "uint8")
+for _n, _w in (("TA", 512), ("TB", 512), ("TR", 1288), ("TW", 512), ("TE", 520), ("TX1", 520), ("TX2", 768)):
+    SCRATCH[_n] = ("sbuf", [128, _w], "bfloat16")
+for _n, _w in (("J", 128), ("CP", 48), ("Z32", 32), ("C115", 32), ("TH0", 80), ("QT", 128), ("GTB", 128),
+               ("GN", 128), ("CM", 128), ("CMI", 128), ("TRI", 32), ("IT", 328), ("NT", 368),
+               ("DH", 8), ("D0", 80), ("C0", 80), ("COL", 32), ("Z0", 64), ("KR0", 128), ("S0", 256),
+               ("G64", 64), ("GT", 64), ("NE", 32), ("D32", 32), ("SAME", 32), ("INVB", 32), ("INVR", 32), ("BASE", 32),
+               ("W32", 32), ("SM", 128), ("THA", 128), ("JK", 128), ("D1", 128), ("CA", 128), ("CB", 128),
+               ("Z1", 64), ("KR1", 128), ("S1", 384), ("BC0", 32), ("BC", 32), ("Z2", 64), ("KR2", 128), ("S2", 384),
+               ("ZP", 32), ("KRP", 32), ("SP", 96), ("NR", 136), ("NM", 384), ("HM", 768), ("Y", 384),
+               ("RES", 4), ("LAND", 12)):
+    SCRATCH[_n] = ("sbuf", [128, _w], "float32")
+SCRATCH["CI"] = ("sbuf", [128, 8], "int32")
+for _n, _w in (("OZ", 8), ("OX", 8), ("OV", 8), ("OE", 8), ("OW", 10), ("OWN", 4)):
+    SCRATCH[_n] = ("sbuf", [128, _w], "uint16")
+SCRATCH["RU"] = ("sbuf", [128, 3, 4], "uint16")
+SCRATCH["FULL"] = ("sbuf", [128, 3, 12], "uint16")
+SCRATCH["PA"] = ("psum", [128, 512], "float32")
+SCRATCH["PB"] = ("psum", [128, 512], "float32")
+SCRATCH["PD"] = ("psum", [128, 2048], "float32")
+SCRATCH["PY"] = ("psum", [128, 1024], "float32")
+
+NPOOL = 142
+SEMAPHORES = ["a0", "a1", "lb", "ce", "locA", "locB"] + ["s%d" % _i for _i in range(NPOOL)]
+
+EPS = 2.0 ** -75
+HUGE = 1e29
+
+
+def rank_program(g, core, T, topo):
+    rank = T.rank_of(core)
+    if rank is None:
+        return
+    N = len(T.cores)
+    A = AluOpType
+    AF = ActivationFunctionType
+    V, S, TE_, SY = g.vector, g.scalar, g.tensor, g.sync
+    Q = {"g": g, "v": V, "a": S, "t": TE_, "s": SY}
+    known = {k: {} for k in Q}
+    total = {}
+    fresh = [0]
+
+    def wait(q, deps):
+        for d in deps:
+            if d is None:
+                continue
+            name, cnt = d
+            if known[q].get(name, 0) < cnt:
+                Q[q].wait_ge(T.sem[name], cnt)
+                known[q][name] = cnt
+
+    def newsem():
+        name = "s%d" % fresh[0]
+        fresh[0] += 1
+        return name
+
+    def R(q, deps, *fns, inc=1):
+        wait(q, deps)
+        name = newsem()
+        for fn in fns:
+            fn().then_inc(T.sem[name], inc)
+        total[name] = inc * len(fns)
+        return (name, total[name])
+
+    def D(q, deps, *pairs):
+        return R(q, deps, *[(lambda o=o, i=i: Q[q].dma_start(o, i)) for o, i in pairs], inc=16)
+
+    def ts(out, in0, s1, s2, op0, op1=None):
+        if op1 is None:
+            return lambda: V.tensor_scalar(out, in0, s1, None, op0)
+        return lambda: V.tensor_scalar(out, in0, s1, s2, op0, op1)
+
+    def tt(out, a, b, op):
+        return lambda: V.tensor_tensor(out, a, b, op)
+
+    def cp(out, a):
+        return lambda: V.tensor_copy(out, a)
+
+    def ms(out, c):
+        return lambda: V.memset(out, c)
+
+    def red(out, a):
+        return lambda: V.tensor_reduce(out, a, AxisListType.X, A.add)
+
+    def rmin(out, a):
+        return lambda: V.tensor_reduce(out, a, AxisListType.X, A.min, apply_absolute_value=True)
+
+    def tr(out, a):
+        return lambda: V.transpose(out, a)
+
+    def act(out, a, func, bias=0.0, scale=1.0):
+        return lambda: S.activation(out, a, func, bias=bias, scale=scale)
+
+    def qz(n, a, b, tile):
+        return lambda: V.quantize_mx(T[n + "c"][:, a:b], T[n + "s"][:, a:b], tile)
+
+    def mm(out, w, wa, x, xa, n, start, stop):
+        return lambda: TE_.matmul_mx(out, T[w + "c"][:, wa:wa + 128], T[w + "s"][:, wa:wa + 128],
+                                     T[x + "c"][:, xa:xa + n], T[x + "s"][:, xa:xa + n], start, stop)
+
+    def pickc(o, oa, n, w, wa, wb, off):
+        return lambda: V.tensor_copy(T[o + "c"][:, oa:oa + n].bitcast(dt.uint32),
+                                     T[w + "c"][:, wa:wb].bitcast(dt.uint32).indirect(off))
+
+    def picks(o, oa, n, w, wa, wb, off):
+        return lambda: S.activation(T[o + "s"][:, oa:oa + n], T[w + "s"][:, wa:wb].indirect(off), AF.Copy)
+
+    def ga(out, win, off):
+        return lambda: S.activation(out, win.indirect(off), AF.Copy)
+
+    def io(out, pat, base, cm):
+        return lambda: g.iota(out, pat, base, cm, allow_small_or_imprecise_dtypes=True)
+
+    def spread(Z, in0, s1, s2):
+        fns = []
+        for (o0, o1, c, i0, i1) in ((0, 128, 0, 0, 128), (0, 64, 32, 64, 128), (64, 128, 32, 0, 64)):
+            fns.append(ts(Z[o0:o1, c:c + 32], in0[i0:i1, 0:32], s1[0][i0:i1, s1[1]:s1[1] + 1],
+                          s2[0][i0:i1, s2[1]:s2[1] + 1], A.add, A.add))
+        return fns
+
+    def turn(KR, Z):
+        fns = [tr(KR[:, 0:64], Z[:, 0:64])]
+        for a in range(4):
+            b = a ^ 1
+            fns.append(tr(KR[32 * a:32 * a + 32, 64:128], Z[32 * b:32 * b + 32, 0:64]))
+        return fns
+
+    peers = [(rank + 1 + s) % N for s in range(N - 1)]
+    ids = []
+    eng = None
+    for d in peers:
+        rid, pid, _se = topo.addr(T.cores[d])
+        ids.append(DstId(rid=rid, pnc=pid))
+        e = topo.engines(core, T.cores[d])
+        eng = e if eng is None else [x for x in eng if x in e]
+
+    def mask(es):
+        m = 0
+        for x in es:
+            m |= 1 << x
+        return m
+    NE_ = len(eng)
+    mall = mask(eng)
+    own_q = [(rank + o) % N for o in range(N)]
+    CP, COL = T.CP, T.COL
+    ID = AF.Identity
+
+    def c1(i):
+        return CP[:, i:i + 1]
+
+    l_r0 = D("s", [], (T.TA[:, 432:512], T.r0[:, :]))
+    l_u = D("a", [], (T.TA[:, 0:8], T.u[:, 0:8]))
+    l_r1 = D("s", [], (T.TB[:, 192:512], T.r1[:, :]))
+    i_p = R("g", [], lambda: g.iota(T.CI[:, 0:1], [[1, 1]], 0, 1))
+    i_j = R("g", [], io(T.J[:, :], [[1, 128]], 0, 0))
+    i_2 = R("g", [], io(T.CMI[:, :], [[1, 4], [4, 32]], 0, 0))
+    f_a = R("v", [], ms(T.TA[:, 8:432], 0.0), ms(T.TB[:, 0:192], 0.0))
+    f_e = R("v", [], ms(T.TE[:, :], 0.0), ms(T.OZ[:, :], 0), ms(T.Z32[:, :], 0.0))
+    k1 = R("v", [i_p],
+           ts(T.CI[:, 1:2], T.CI[:, 0:1], 15, None, A.bitwise_and),
+           ts(T.CI[:, 2:3], T.CI[:, 0:1], 5, None, A.logical_shift_right),
+           ts(T.CI[:, 3:4], T.CI[:, 0:1], 31, None, A.bitwise_and),
+           ts(T.CI[:, 4:5], T.CI[:, 0:1], 15, 2, A.bitwise_and, A.logical_shift_right),
+           ts(T.CI[:, 5:6], T.CI[:, 0:1], 3, None, A.bitwise_and))
+    k2 = R("v", [k1], cp(CP[:, 0:6], T.CI[:, 0:6]))
+    k3 = R("v", [k2, i_j, f_e],
+           ts(T.TE[:, 3:515:4], T.J[:, :], c1(0), None, A.is_equal),
+           ts(CP[:, 32:33], c1(0), 127.5 - 20 * rank, -80.0, A.is_gt, A.mult),
+           ts(CP[:, 33:34], c1(0), 47.5, 1000.0, A.is_lt, A.mult),
+           ts(CP[:, 35:36], c1(2), 64.0, c1(4), A.mult, A.add),
+           ts(CP[:, 36:37], c1(3), 4.0, c1(2), A.mult, A.add))
+    k3a = R("a", [k2, i_j],
+            act(CP[:, 6:8], T.J[:, 0:32:16], ID, bias=c1(1)),
+            act(CP[:, 24:28], T.J[:, 0:4], ID, bias=-4.0 / 512, scale=0.0),
+            act(CP[:, 28:32], T.J[:, 0:4], ID, bias=-144.0 / 2048, scale=1.0 / 2048),
+            act(CP[:, 21:22], c1(1), ID, bias=-16.0, scale=-1.0),
+            act(CP[:, 22:23], c1(3), ID, bias=-0.5),
+            act(CP[:, 37:38], c1(2), ID, scale=1.0 / 256),
+            act(CP[:, 38:39], c1(3), ID, scale=1.0 / 512),
+            act(CP[:, 39:40], c1(0), ID, scale=1.0 / 512),
+            act(CP[:, 11:12], c1(5), ID, scale=-1.0 / 1024),
+            act(CP[:, 15:16], c1(5), ID, scale=-32.0 / 512))
+
+    q_a = R("v", [l_r0, l_u, f_a], qz("P0", 0, 128, T.TA[:, :]))
+    q_b = R("v", [l_r1], qz("P1", 0, 128, T.TB[:, :]))
+
+    def bcast(src, dsts, sem, loc):
+        g.remote_dma_fused([RemoteDMATransfer(dst_ids=ids, dma_engine_mask=mall, remote_sem=T.sem[sem],
+                                              srcs=[src], dsts=dsts)], local_sem=T.sem[loc])
+    at = [(rank - d) % N - 1 for d in peers]
+    wait("g", [q_a])
+    bcast(T.P0c[:, 108:128].bitcast(dt.uint8), [T.P0c[:, 128 + 20 * o:148 + 20 * o].bitcast(dt.uint8) for o in at], "a0", "locA")
+    bcast(T.P0s[:, 108:128], [T.P0s[:, 128 + 20 * o:148 + 20 * o] for o in at], "a0", "locA")
+    wait("g", [q_b])
+    bcast(T.P1c[:, 48:128].bitcast(dt.uint8), [T.P1c[:, 128 + 80 * o:208 + 80 * o].bitcast(dt.uint8) for o in at], "a1", "locA")
+    bcast(T.P1s[:, 48:128], [T.P1s[:, 128 + 80 * o:208 + 80 * o] for o in at], "a1", "locA")
+    a0 = ("a0", 2 * (N - 1) * NE_)
+    a1 = ("a1", 2 * (N - 1) * NE_)
+    locA = ("locA", 4 * NE_)
+    l_r2 = D("s", [locA], (T.TR[:, 0:1280], T.r2[:, :]))
+    l_w = D("s", [], (T.TW[:, :], T.w[:, :]))
+    i_3 = R("g", [], io(T.IT[:, 0:320], [[1, 320]], 0, 0), io(T.NT[:, 48:368], [[0, 4], [1, 80]], 0, 0))
+
+    p_uc = R("v", [f_e, q_a], pickc("UR", 0, 128, "P0", 0, 32, T.OZ[:, 0:8]))
+    p_us = R("a", [f_e, q_a], picks("UR", 0, 128, "P0", 0, 32, T.OZ[:, 0:8]))
+    k4 = R("v", [k3],
+           ts(CP[:, 20:21], c1(0), 20.0 * rank - 48, c1(32), A.add, A.add),
+           ts(CP[:, 34:35], c1(0), 1.0 / 512, c1(33), A.mult, A.add))
+    q_e = R("v", [k3], *[qz("E", 128 * b, 128 * b + 128, T.TE[:, 3 - b:515 - b]) for b in range(4)])
+    m_h = R("t", [q_e, q_a], *[mm(T.PD[:, 512 * b:512 * b + 128], "E", 128 * b, "P0", 0, 128, True, True) for b in range(4)])
+    k4b = R("v", [k4],
+            ts(CP[:, 40:41], c1(20), -20.0 * rank, None, A.add),
+            ts(CP[:, 41:42], c1(20), 80.0 - 20.0 * rank, None, A.add))
+    cut = 80 - 20 * rank
+    k6 = R("v", [k3a],
+           ts(CP[:, 12:15], T.J[:, 0:12:4], c1(35), None, A.add),
+           ts(CP[:, 8:11], T.J[:, 0:12:4], c1(35), c1(11), A.add, A.add),
+           ts(CP[:, 16:19], T.J[:, 0:12:4], c1(35), c1(15), A.add, A.add),
+           ts(T.OX[:, 0:8:2], T.Z32[:, 0:4], c1(6), None, A.add),
+           ts(T.OX[:, 1:8:2], T.Z32[:, 0:4], c1(7), None, A.add))
+    k5 = R("v", [k4b], ts(T.TH0[:, 0:cut], T.J[:, 0:cut], c1(40), EPS, A.subtract, A.mult),
+           *([ts(T.TH0[:, cut:80], T.J[:, cut:80], c1(41), EPS, A.subtract, A.mult)] if rank else []))
+    seg = [(0, 64), (64, 84), (84, 104), (104, 128)]
+    k6a = R("a", [k3a],
+            act(T.GN[:, :], T.J[:, :], ID, bias=c1(37), scale=1.0 / 64),
+            act(T.TRI[:, :], T.J[:, 0:32], ID, bias=c1(22), scale=-1.0),
+            act(T.C115[:, :], T.J[:, 0:32], ID, bias=11.5, scale=0.0),
+            act(T.NT[:, 0:48], T.J[:, 0:48], ID, scale=0.0),
+            act(T.IT[:, 320:328], T.J[:, 0:8], ID, bias=-1.0, scale=0.0),
+            act(T.NR[:, 128:136], T.J[:, 0:8], ID, bias=-1.0, scale=0.0))
+    k7a = R("a", [k6a, k6],
+            act(CP[:, 42:45], CP[:, 8:11], ID, scale=-1.0), act(CP[:, 45:48], CP[:, 12:15], ID, scale=-1.0),
+            *[act(T.GTB[:, seg[o][0]:seg[o][1]], T.GN[:, seg[o][0]:seg[o][1]], ID, bias=64.0 * own_q[o] - (44 + 20 * o) / 64)
+              for o in range(N)])
+    c_h = R("a", [m_h], act(T.DH[:, 0:4], T.PD[:, 1:2048:512], AF.Copy))
+    k7 = R("v", [i_2],
+           ts(T.CM[:, :], T.CMI[:, :], c1(36), EPS, A.subtract, A.mult),
+           ms(T.TR[:, 1280:1288], 0.0), ms(T.TX1[:, 512:520], 0.0),
+           *[ms(T.QT[:, seg[o][0]:seg[o][1]], EPS * 128 * own_q[o]) for o in range(N)])
+
+    m_r0 = R("t", [a0, p_uc, p_us], mm(T.PA[:, 0:128], "UR", 0, "P0", 60, 128, True, True),
+             mm(T.PB[:, 0:128], "P0", 60, "P0", 0, 128, True, True))
+    x = d0 = R("v", [m_r0], ts(T.D0[:, :], T.PA[:, 48:128], T.PB[:, 0:1], None, A.subtract))
+    x = R("v", [x, k5], tt(T.C0[:, :], T.D0[:, :], T.TH0[:, :], A.is_gt))
+    x = R("v", [x], red(COL[:, 0:1], T.C0[:, :]))
+    x = R("v", [x], *spread(T.Z0, T.Z32, (COL, 0), (CP, 34)))
+    kr0 = R("v", [x], *turn(T.KR0, T.Z0))
+    sa = R("a", [kr0], act(T.S0[:, 128:256], T.KR0[:, :], AF.Abs, bias=c1(21)))
+    x = R("v", [kr0], ts(T.S0[:, 0:128], T.KR0[:, :], c1(6), None, A.subtract))
+    f0 = R("v", [x], rmin(COL[:, 1:2], T.S0[:, 0:128]))
+    f1 = R("v", [sa], rmin(COL[:, 2:3], T.S0[:, 128:256]))
+    o_v = R("v", [f0, f1], *[ts(T.OV[:, h:8:2], CP[:, 24:28], COL[:, 1 + h:2 + h], 512.0, A.add, A.mult) for h in range(2)])
+    o_e = R("v", [], *[ts(T.OE[:, h:8:2], CP[:, 28:32], COL[:, 1 + h:2 + h], 2048.0, A.add, A.mult) for h in range(2)])
+    p_vc = R("v", [o_v, a0], pickc("V1", 0, 128, "P0", 64, 188, T.OV[:, 0:8]))
+    m1 = R("a", [o_v, k7, k7a], ga(T.G64[:, 0:32], T.GTB[:, :], T.OV[:, 0:2]), ga(T.G64[:, 32:64], T.QT[:, :], T.OV[:, 0:2]))
+    p_vs = R("a", [a0], picks("V1", 0, 128, "P0", 64, 188, T.OV[:, 0:8]))
+    p_es = R("a", [o_e, a1, q_b], picks("E1", 0, 128, "P1", 0, 368, T.OE[:, 0:8]))
+    m2 = R("v", [m1], tr(T.GT[:, :], T.G64[:, :]))
+    qc = T.GT[:, 32:33]
+    m3 = R("v", [m2], ts(T.NE[:, :], T.G64[:, 32:64], qc, HUGE, A.not_equal, A.mult),
+           ts(T.D32[:, :], T.G64[:, 32:64], qc, None, A.subtract))
+    p_ec = R("v", [o_e, a1, q_b], pickc("E1", 0, 128, "P1", 0, 368, T.OE[:, 0:8]))
+    wait("t", [p_vc, p_vs, c_h])
+    for b in range(4):
+        mm(T.PD[:, 512 * b:512 * b + 128], "E", 128 * b, "V1", 0, 128, True, False)()
+    m_e = [R("t", [p_ec, p_es], mm(T.PD[:, 512 * b:512 * b + 128], "E", 128 * b, "E1", 0, 128, False, True)) for b in range(4)]
+    m4 = R("v", [m3, k6a], tt(T.SAME[:, :], T.NE[:, :], T.TRI[:, :], A.is_lt))
+    m5 = R("v", [m4], red(COL[:, 3:4], T.SAME[:, :]))
+    m6 = R("v", [m5], ts(T.INVB[:, :], T.C115[:, :], COL[:, 3:4], HUGE, A.is_lt, A.mult))
+    cs = []
+    for b in range(2):
+        cs.append(R("a", [m_e[b], c_h], act(T.TX1[:, b:512:4], T.PD[:, 512 * b:512 * b + 128], ID, bias=T.DH[:, b:b + 1])))
+    m7 = R("v", [m6], tr(T.INVR[:, :], T.INVB[:, :]), tt(T.BASE[:, :], T.GT[:, 0:32], T.INVB[:, :], A.add))
+    cs.append(R("v", [m_e[3], m_e[2], c_h], *[ts(T.TX1[:, b:512:4], T.PD[:, 512 * b:512 * b + 128], T.DH[:, b:b + 1], None, A.add)
+                                              for b in (2, 3)]))
+    m8 = R("v", [m7], tt(T.W32[:, :], T.D32[:, :], T.INVR[:, :], A.add))
+    q_x1 = R("v", cs, qz("X1", 0, 130, T.TX1[:, :]))
+    m_r1 = R("t", [q_x1, d0], mm(T.PA[:, 0:128], "UR", 0, "X1", 0, 128, True, True),
+             mm(T.PB[:, 0:128], "X1", 0, "P0", 0, 128, True, True))
+    sm0 = R("a", [m3, k6], lambda: S.activation(T.JK[:, :], T.D32[:, :].indirect(T.OX[:, 0:8]), AF.Abs, scale=2.0 ** 68))
+    sm = R("a", [sm0], act(T.SM[:, :], T.JK[:, :], AF.Relu, bias=1.0, scale=-1.0))
+    m9 = R("v", [m8, k6], tt(T.THA[:, :], T.W32[:, :].indirect(T.OX[:, 0:8]), T.CM[:, :], A.add))
+
+    d1 = R("v", [m_r1], ts(T.D1[:, :], T.PA[:, 0:128], T.PB[:, 0:1], None, A.subtract))
+    ca = R("v", [d1, m9], tt(T.CA[:, :], T.D1[:, :], T.THA[:, :], A.is_gt))
+    ra = R("a", [ca, sm], lambda: S.activation(T.JK[:, :], T.CA[:, :], AF.Copy, accum_out=COL[:, 4:5]))
+    cb = R("v", [ca, sm], tt(T.CB[:, :], T.CA[:, :], T.SM[:, :], A.mult))
+    tf = R("a", [ra], act(COL[:, 6:7], COL[:, 4:5], AF.Relu, bias=-31.0 * 1024, scale=1024.0))
+    rb = R("v", [cb], red(COL[:, 5:6], T.CB[:, :]))
+    x = R("v", [rb, tf], *spread(T.Z1, T.BASE, (COL, 5), (COL, 6)))
+    kr1 = R("v", [x], *turn(T.KR1, T.Z1))
+    sb = [R("a", [kr1], act(T.S1[:, 128 * j:128 * j + 128], T.KR1[:, :], AF.Abs, bias=c1(42 + j))) for j in (1, 2)]
+    x = R("v", [kr1], ts(T.S1[:, 0:128], T.KR1[:, :], c1(8), None, A.subtract))
+    r_e = [R("v", [d], rmin(T.RES[:, j:j + 1], T.S1[:, 128 * j:128 * j + 128])) for j, d in enumerate([x] + sb)]
+
+    wait("g", r_e)
+    bcast(T.RES[:, 0:3], [T.LAND[:, 3 * o:3 * o + 3] for o in at], "lb", "locB")
+    lb = ("lb", (N - 1) * NE_)
+
+    q_r2 = R("v", [l_r2], qz("R2", 0, 322, T.TR[:, :]))
+    n_r = R("a", [i_3], ga(T.NR[:, 0:128], T.NT[:, :], T.OE[:, 0:8]))
+    b0 = R("v", r_e, ts(T.BC0[:, :], T.GT[:, 32:64], 2.0 ** 74, c1(39), A.mult, A.add),
+           ts(COL[:, 7:8], COL[:, 3:4], c1(38), None, A.add),
+           ts(T.RU[:, 0, 0:3], T.RES[:, 0:3], 1024.0, 320.0, A.mult, A.min))
+    x = R("v", [b0], tt(T.BC[:, :], T.BC0[:, :], T.INVB[:, :], A.add),
+          ts(T.ZP[:, :], T.GT[:, 32:64], 2.0 ** 74, COL[:, 7:8], A.mult, A.add))
+    x = R("v", [x], tr(T.KRP[:, :], T.ZP[:, :]), *spread(T.Z2, T.BC, (COL, 5), (COL, 6)))
+    kr2 = R("v", [x], *(turn(T.KR2, T.Z2) +
+                        [ts(T.SP[:, 32 * j:32 * j + 32], T.KRP[:, :], c1(16 + j), None, A.subtract) for j in range(3)]))
+    xs = R("a", [kr2], *[act(T.S2[:, 128 * j:128 * j + 128], T.KR2[:, :], AF.Abs, bias=c1(45 + j)) for j in range(3)])
+
+    x = R("v", [lb], *[ts(T.OW[32 * a:32 * a + 32, 0:9], T.LAND[32 * rank:32 * rank + 32, 0:9], 1024.0, 320.0, A.mult, A.min)
+                       for a in range(4)])
+    s_c = R("v", [x, q_r2], pickc("SN", 0, 144, "R2", 0, 322, T.OW[:, 0:9]))
+    s_s = R("a", [x, q_r2], picks("SN", 0, 144, "R2", 0, 322, T.OW[:, 0:9]))
+    u = NE_ // 4
+    mc = [mask(eng[0:u]), mask(eng[u:2 * u]), mask(eng[2 * u:])]
+    msk = [mask(eng[0:2 * u]), mask(eng[2 * u:3 * u]), mask(eng[3 * u:])]
+    wait("g", [s_c])
+    g.remote_dma_fused([RemoteDMATransfer(dst_ids=[ids[s]], dma_engine_mask=mc[s], remote_sem=T.sem.ce,
+                                          src=T.SNc[:, 48 * s:48 * s + 48].bitcast(dt.uint8),
+                                          dst=T.E2c[:, 48 * rank:48 * rank + 48].bitcast(dt.uint8)) for s in range(N - 1)],
+                       local_sem=T.sem.locB)
+    wait("g", [s_s])
+    g.remote_dma_fused([RemoteDMATransfer(dst_ids=[ids[s]], dma_engine_mask=msk[s], remote_sem=T.sem.ce,
+                                          src=T.SNs[:, 48 * s:48 * s + 48],
+                                          dst=T.E2s[:, 48 * rank:48 * rank + 48]) for s in range(N - 1)],
+                       local_sem=T.sem.locB)
+    ce = ("ce", 2 * NE_)
+    locB = ("locB", 3 * NE_)
+
+    x = R("v", [xs], *([rmin(COL[:, 12 + j:13 + j], T.S2[:, 128 * j:128 * j + 128]) for j in range(3)] +
+                       [rmin(COL[:, 16 + j:17 + j], T.SP[:, 32 * j:32 * j + 32]) for j in range(3)]))
+    x = R("v", [x], ts(T.RU[:, 1, 0:3], COL[:, 12:15], 512.0, 128.0, A.mult, A.min),
+          ts(T.RU[:, 2, 0:3], COL[:, 16:19], 512.0, 128.0, A.mult, A.min))
+    ow = R("v", [b0], *[cp(T.OWN[32 * a:32 * a + 32, 0:3], T.RU[32 * rank:32 * rank + 32, 0, 0:3]) for a in range(4)])
+    fu = R("v", [x], *[cp(T.FULL[32 * a:32 * a + 32, :, 3 * q:3 * q + 3], T.RU[32 * q:32 * q + 32, :, 0:3])
+                       for q in range(N) for a in range(4)])
+    e2s = R("a", [ow], picks("E2", 48 * rank, 48, "R2", 0, 322, T.OWN[:, 0:3]))
+    n2 = R("a", [fu, i_3], ga(T.NM[:, 192:384], T.IT[:, :], T.FULL[:, 0, :]))
+    e2c = R("v", [ow], pickc("E2", 48 * rank, 48, "R2", 0, 322, T.OWN[:, 0:3]))
+    v2c = R("v", [fu], pickc("V2", 0, 192, "X1", 0, 130, T.FULL[:, 1, :]))
+    v2s = R("a", [q_x1], picks("V2", 0, 192, "X1", 0, 130, T.FULL[:, 1, :]))
+    o1s = R("a", [], picks("O1", 0, 192, "X1", 0, 130, T.FULL[:, 2, :]))
+    o1c = R("v", [], pickc("O1", 0, 192, "X1", 0, 130, T.FULL[:, 2, :]))
+    hm = R("v", [n2], *[ts(T.HM[:, 192 * b:192 * b + 192], T.NM[:, 192:384], -0.5, T.DH[:, b:b + 1], A.is_gt, A.mult)
+                        for b in range(4)])
+    q_w = R("v", [l_w], qz("W", 0, 128, T.TW[:, :]))
+    n1 = R("a", [n_r], ga(T.NM[:, 0:192], T.NR[:, :], T.FULL[:, 2, :]))
+    wait("t", [v2c, v2s] + cs)
+    for b in range(4):
+        mm(T.PD[:, 512 * b:512 * b + 192], "E", 128 * b, "V2", 0, 192, True, False)()
+    m_y0 = R("t", [o1c, o1s, q_w], mm(T.PY[:, 0:192], "W", 0, "O1", 0, 192, True, True))
+    c_y0 = R("a", [m_y0], act(T.Y[:, 0:192], T.PY[:, 0:192], AF.Copy))
+    D("s", [n1, n2], (T.nm[:, :], T.NM[0:1, :]))
+    D("s", [c_y0, locB], (T.y[:, 0:192], T.Y[:, 0:192]))
+
+    m_e2 = [R("t", [ce, e2c, e2s], mm(T.PD[:, 512 * b:512 * b + 192], "E", 128 * b, "E2", 0, 192, False, True)) for b in range(4)]
+    name = newsem()
+    for b in range(4):
+        wait("v", [hm, m_e2[b]])
+        tt(T.TX2[:, b:768:4], T.PD[:, 512 * b:512 * b + 192], T.HM[:, 192 * b:192 * b + 192], A.add)().then_inc(T.sem[name], 1)
+    total[name] = 4
+    q_x2 = R("v", [(name, 4)], qz("X2", 0, 192, T.TX2[:, :]))
+    m_y1 = R("t", [q_x2], mm(T.PY[:, 512:704], "W", 0, "X2", 0, 192, True, True))
+    c_y1 = R("v", [m_y1], cp(T.Y[:, 192:384], T.PY[:, 512:704]))
+    D("s", [q_x2], (T.oc[:, :], T.X2c[:, 0:192].bitcast(dt.uint8)),
+      *[(T.osc[4 * k:4 * k + 4, :], T.X2s[32 * k:32 * k + 4, 0:192]) for k in range(2)])
+    D("a", [q_x2], *[(T.osc[4 * k:4 * k + 4, :], T.X2s[32 * k:32 * k + 4, 0:192]) for k in range(2, 4)])
+    D("a", [c_y1], (T.y[:, 192:384], T.Y[:, 192:384]))
+
+    for name in total:
+        if max(known[q].get(name, 0) for q in known) < total[name]:
+            wait("g", [(name, total[name])])

@@ -3,33 +3,34 @@ from concourse.mybir import dt, AluOpType, AxisListType, ActivationFunctionType
 
 FP8 = "float8_e4m3fn_x4"
 SCRATCH = {}
-for _n, _w in (("P0", 188), ("P1", 368), ("R2", 322), ("W", 128), ("E", 512), ("UR", 128), ("V1", 128), ("E1", 128),
-               ("X1", 130), ("O1", 192), ("V2", 192), ("E2", 192), ("SN", 144), ("X2", 192)):
+for _n, _w in (("L0", 194), ("R4", 234), ("UR", 128), ("UO", 128), ("E", 512), ("RR", 128), ("R1", 128), ("R2", 320),
+               ("X1", 336), ("P1", 208), ("LP1", 192), ("V2", 192), ("E2", 192), ("X2", 192), ("LP2", 208),
+               ("XF", 192), ("W", 128)):
     SCRATCH[_n + "c"] = ("sbuf", [128, _w], FP8)
     SCRATCH[_n + "s"] = ("sbuf", [128, _w], "uint8")
-for _n, _w in (("TA", 512), ("TB", 512), ("TR", 1288), ("TW", 512), ("TE", 520), ("TX1", 520), ("TX2", 768)):
+for _n, _w in (("TA", 936), ("TB", 512), ("TR", 1280), ("TW", 512), ("TE", 520), ("TX1", 1344), ("TX2", 768)):
     SCRATCH[_n] = ("sbuf", [128, _w], "bfloat16")
-for _n, _w in (("J", 128), ("CP", 48), ("Z32", 32), ("C115", 32), ("TH0", 80), ("QT", 128), ("GTB", 128),
-               ("GN", 128), ("CM", 128), ("CMI", 128), ("TRI", 32), ("IT", 328), ("NT", 368),
-               ("DH", 8), ("D0", 80), ("C0", 80), ("COL", 32), ("Z0", 64), ("KR0", 128), ("S0", 256),
-               ("G64", 64), ("GT", 64), ("NE", 32), ("D32", 32), ("SAME", 32), ("INVB", 32), ("INVR", 32), ("BASE", 32),
-               ("W32", 32), ("SM", 128), ("THA", 128), ("JK", 128), ("D1", 128), ("CA", 128), ("CB", 128),
-               ("Z1", 64), ("KR1", 128), ("S1", 384), ("BC0", 32), ("BC", 32), ("Z2", 64), ("KR2", 128), ("S2", 384),
-               ("ZP", 32), ("KRP", 32), ("SP", 96), ("NR", 136), ("NM", 384), ("HM", 768), ("Y", 384),
-               ("RES", 4), ("LAND", 12)):
+for _n, _w in (("J", 128), ("CP", 32), ("ZB", 160), ("DJ", 48), ("TH0", 88), ("THS", 96), ("XT", 64),
+               ("BI", 64), ("AB", 32), ("TQ", 8), ("W0", 96), ("WS", 96), ("RS", 128), ("IT", 336), ("NT", 336),
+               ("PT", 336), ("KT", 208), ("S1", 320), ("DH", 16), ("D0", 88), ("C0", 96), ("SA", 96), ("M0", 96), ("MT0", 96),
+               ("SC0", 96), ("NP", 128), ("NPT", 128), ("TH1", 96), ("ZT", 64), ("RA", 64), ("D1", 96),
+               ("C1", 96), ("MT1", 192), ("ML", 16), ("CL", 16), ("LIM", 8), ("PA1", 192), ("RM", 192),
+               ("F", 384), ("JK", 192), ("O2", 8), ("FG", 8), ("Z2", 64), ("KR", 128), ("SCN", 128), ("FA", 16), ("FB", 16),
+               ("NR", 208), ("MK", 192), ("NM", 384), ("Y", 384)):
     SCRATCH[_n] = ("sbuf", [128, _w], "float32")
+SCRATCH["IO"] = ("sbuf", [128, 3, 32], "float32")
+SCRATCH["M1"] = ("sbuf", [128, 3, 64], "float32")
 SCRATCH["CI"] = ("sbuf", [128, 8], "int32")
-for _n, _w in (("OZ", 8), ("OX", 8), ("OV", 8), ("OE", 8), ("OW", 10), ("OWN", 4)):
+for _n, _w in (("OZ", 8), ("OU", 8), ("OR", 8), ("OX", 8), ("OL", 8), ("O0", 16), ("OV", 16), ("OE", 16), ("FL", 16),
+               ("LL0", 16), ("LL1", 16)):
     SCRATCH[_n] = ("sbuf", [128, _w], "uint16")
-SCRATCH["RU"] = ("sbuf", [128, 3, 4], "uint16")
-SCRATCH["FULL"] = ("sbuf", [128, 3, 12], "uint16")
 SCRATCH["PA"] = ("psum", [128, 512], "float32")
 SCRATCH["PB"] = ("psum", [128, 512], "float32")
 SCRATCH["PD"] = ("psum", [128, 2048], "float32")
 SCRATCH["PY"] = ("psum", [128, 1024], "float32")
 
-NPOOL = 142
-SEMAPHORES = ["a0", "a1", "lb", "ce", "locA", "locB"] + ["s%d" % _i for _i in range(NPOOL)]
+NPOOL = 138
+SEMAPHORES = ["ac", "asc", "l0", "p1", "ms", "l1", "p2c", "p2s", "locA", "locB"] + ["s%d" % _i for _i in range(NPOOL)]
 
 EPS = 2.0 ** -75
 HUGE = 1e29
@@ -46,6 +47,7 @@ def rank_program(g, core, T, topo):
     Q = {"g": g, "v": V, "a": S, "t": TE_, "s": SY}
     known = {k: {} for k in Q}
     total = {}
+    home = {}
     fresh = [0]
 
     def wait(q, deps):
@@ -57,17 +59,22 @@ def rank_program(g, core, T, topo):
                 Q[q].wait_ge(T.sem[name], cnt)
                 known[q][name] = cnt
 
-    def newsem():
-        name = "s%d" % fresh[0]
-        fresh[0] += 1
-        return name
-
     def R(q, deps, *fns, inc=1):
         wait(q, deps)
-        name = newsem()
+        name = None
+        if inc == 1:
+            for n in total:
+                if home[n] == q and known[q].get(n, 0) == total[n]:
+                    name = n
+                    break
+        if name is None:
+            name = "s%d" % fresh[0]
+            fresh[0] += 1
+            total[name] = 0
+            home[name] = q if inc == 1 else None
         for fn in fns:
             fn().then_inc(T.sem[name], inc)
-        total[name] = inc * len(fns)
+        total[name] += inc * len(fns)
         return (name, total[name])
 
     def D(q, deps, *pairs):
@@ -90,8 +97,8 @@ def rank_program(g, core, T, topo):
     def red(out, a):
         return lambda: V.tensor_reduce(out, a, AxisListType.X, A.add)
 
-    def rmin(out, a):
-        return lambda: V.tensor_reduce(out, a, AxisListType.X, A.min, apply_absolute_value=True)
+    def scan(out, d0, d1):
+        return lambda: V.tensor_tensor_scan(out, d0, d1, 0.0, A.mult, A.add)
 
     def tr(out, a):
         return lambda: V.transpose(out, a)
@@ -119,27 +126,21 @@ def rank_program(g, core, T, topo):
     def io(out, pat, base, cm):
         return lambda: g.iota(out, pat, base, cm, allow_small_or_imprecise_dtypes=True)
 
-    def spread(Z, in0, s1, s2):
-        fns = []
-        for (o0, o1, c, i0, i1) in ((0, 128, 0, 0, 128), (0, 64, 32, 64, 128), (64, 128, 32, 0, 64)):
-            fns.append(ts(Z[o0:o1, c:c + 32], in0[i0:i1, 0:32], s1[0][i0:i1, s1[1]:s1[1] + 1],
-                          s2[0][i0:i1, s2[1]:s2[1] + 1], A.add, A.add))
-        return fns
+    def u8(n, a, b):
+        return T[n][:, a:b].bitcast(dt.uint8)
 
-    def turn(KR, Z):
-        fns = [tr(KR[:, 0:64], Z[:, 0:64])]
-        for a in range(4):
-            b = a ^ 1
-            fns.append(tr(KR[32 * a:32 * a + 32, 64:128], Z[32 * b:32 * b + 32, 0:64]))
-        return fns
+    def quad(a):
+        return slice(32 * a, 32 * a + 32)
+    LO, HI, ALL = slice(0, 64), slice(64, 128), slice(0, 128)
 
-    peers = [(rank + 1 + s) % N for s in range(N - 1)]
+    peer = [rank ^ s for s in range(N)]
+    far = list(range(1, N))
     ids = []
     eng = None
-    for d in peers:
-        rid, pid, _se = topo.addr(T.cores[d])
+    for s in far:
+        rid, pid, _se = topo.addr(T.cores[peer[s]])
         ids.append(DstId(rid=rid, pnc=pid))
-        e = topo.engines(core, T.cores[d])
+        e = topo.engines(core, T.cores[peer[s]])
         eng = e if eng is None else [x for x in eng if x in e]
 
     def mask(es):
@@ -148,235 +149,256 @@ def rank_program(g, core, T, topo):
             m |= 1 << x
         return m
     NE_ = len(eng)
-    mall = mask(eng)
-    own_q = [(rank + o) % N for o in range(N)]
-    CP, COL = T.CP, T.COL
+    u = NE_ // 4
+    m_a = [mask(eng[0:u]), mask(eng[u:2 * u]), mask(eng[2 * u:])]
+    m_b = [mask(eng[0:2 * u]), mask(eng[2 * u:3 * u]), mask(eng[3 * u:])]
+
+    def bcast(src, dsts, m, sem, loc):
+        g.remote_dma_fused([RemoteDMATransfer(dst_ids=ids, dma_engine_mask=m, remote_sem=T.sem[sem],
+                                              srcs=[src], dsts=dsts)], local_sem=T.sem[loc])
+
+    def deal(srcs, dst, masks, sem):
+        g.remote_dma_fused([RemoteDMATransfer(dst_ids=[ids[s]], dma_engine_mask=masks[s], remote_sem=T.sem[sem],
+                                              src=srcs[s], dst=dst) for s in range(N - 1)], local_sem=T.sem.locB)
+
+    CP, J, DH, ZB = T.CP, T.J, T.DH, T.ZB
     ID = AF.Identity
+    cq = [106 + 22 * s for s in range(N)]
+    G0, G1, Z0 = 64, 96, 128
 
     def c1(i):
         return CP[:, i:i + 1]
 
+    def fill(out, n, c):
+        return act(out, J[:, 0:n], ID, bias=c, scale=0.0)
+
     l_r0 = D("s", [], (T.TA[:, 432:512], T.r0[:, :]))
-    l_u = D("a", [], (T.TA[:, 0:8], T.u[:, 0:8]))
-    l_r1 = D("s", [], (T.TB[:, 192:512], T.r1[:, :]))
+    l_u = D("a", [], (T.TA[:, 424:432], T.u[:, 0:8]))
+    l_r1 = D("s", [], (T.TB[:, 0:320], T.r1[:, :]))
+    l_r2 = D("s", [], (T.TR[:, :], T.r2[:, :]))
+    l_w = D("s", [], (T.TW[:, :], T.w[:, :]))
     i_p = R("g", [], lambda: g.iota(T.CI[:, 0:1], [[1, 1]], 0, 1))
-    i_j = R("g", [], io(T.J[:, :], [[1, 128]], 0, 0))
-    i_2 = R("g", [], io(T.CMI[:, :], [[1, 4], [4, 32]], 0, 0))
-    f_a = R("v", [], ms(T.TA[:, 8:432], 0.0), ms(T.TB[:, 0:192], 0.0))
-    f_e = R("v", [], ms(T.TE[:, :], 0.0), ms(T.OZ[:, :], 0), ms(T.Z32[:, :], 0.0))
+    i_j = R("g", [], io(J[:, :], [[1, 128]], 0, 0))
+    f_a = R("v", [], ms(T.TA[:, 0:424], 0.0))
+    f_x = R("v", [], ms(ZB[:, :], 0.0))
     k1 = R("v", [i_p],
            ts(T.CI[:, 1:2], T.CI[:, 0:1], 15, None, A.bitwise_and),
            ts(T.CI[:, 2:3], T.CI[:, 0:1], 5, None, A.logical_shift_right),
            ts(T.CI[:, 3:4], T.CI[:, 0:1], 31, None, A.bitwise_and),
            ts(T.CI[:, 4:5], T.CI[:, 0:1], 15, 2, A.bitwise_and, A.logical_shift_right),
            ts(T.CI[:, 5:6], T.CI[:, 0:1], 3, None, A.bitwise_and))
+    f_e = R("v", [], ms(T.TE[:, :], 0.0))
     k2 = R("v", [k1], cp(CP[:, 0:6], T.CI[:, 0:6]))
-    k3 = R("v", [k2, i_j, f_e],
-           ts(T.TE[:, 3:515:4], T.J[:, :], c1(0), None, A.is_equal),
-           ts(CP[:, 32:33], c1(0), 127.5 - 20 * rank, -80.0, A.is_gt, A.mult),
-           ts(CP[:, 33:34], c1(0), 47.5, 1000.0, A.is_lt, A.mult),
-           ts(CP[:, 35:36], c1(2), 64.0, c1(4), A.mult, A.add),
-           ts(CP[:, 36:37], c1(3), 4.0, c1(2), A.mult, A.add))
-    k3a = R("a", [k2, i_j],
-            act(CP[:, 6:8], T.J[:, 0:32:16], ID, bias=c1(1)),
-            act(CP[:, 24:28], T.J[:, 0:4], ID, bias=-4.0 / 512, scale=0.0),
-            act(CP[:, 28:32], T.J[:, 0:4], ID, bias=-144.0 / 2048, scale=1.0 / 2048),
-            act(CP[:, 21:22], c1(1), ID, bias=-16.0, scale=-1.0),
-            act(CP[:, 22:23], c1(3), ID, bias=-0.5),
-            act(CP[:, 37:38], c1(2), ID, scale=1.0 / 256),
-            act(CP[:, 38:39], c1(3), ID, scale=1.0 / 512),
-            act(CP[:, 39:40], c1(0), ID, scale=1.0 / 512),
-            act(CP[:, 11:12], c1(5), ID, scale=-1.0 / 1024),
-            act(CP[:, 15:16], c1(5), ID, scale=-32.0 / 512))
+    f_b = R("v", [], ms(T.TA[:, 512:936], 0.0), ms(T.TB[:, 320:512], 0.0), ms(T.OU[:, :], 10), ms(T.OL[:, :], 0))
+    i_z = R("g", [], io(T.BI[:, 48:56], [[22, 4], [0, 2]], 10, 0))
+    i_o = R("g", [], *[io(T.IO[:, c, :], [[0, 2], [1, 4], [0, 4]], 4 * c, 0) for c in range(3)])
+    q_a = R("v", [l_r0, l_u, f_a], qz("L0", 0, 128, T.TA[:, 0:512]))
 
-    q_a = R("v", [l_r0, l_u, f_a], qz("P0", 0, 128, T.TA[:, :]))
-    q_b = R("v", [l_r1], qz("P1", 0, 128, T.TB[:, :]))
-
-    def bcast(src, dsts, sem, loc):
-        g.remote_dma_fused([RemoteDMATransfer(dst_ids=ids, dma_engine_mask=mall, remote_sem=T.sem[sem],
-                                              srcs=[src], dsts=dsts)], local_sem=T.sem[loc])
-    at = [(rank - d) % N - 1 for d in peers]
     wait("g", [q_a])
-    bcast(T.P0c[:, 108:128].bitcast(dt.uint8), [T.P0c[:, 128 + 20 * o:148 + 20 * o].bitcast(dt.uint8) for o in at], "a0", "locA")
-    bcast(T.P0s[:, 108:128], [T.P0s[:, 128 + 20 * o:148 + 20 * o] for o in at], "a0", "locA")
-    wait("g", [q_b])
-    bcast(T.P1c[:, 48:128].bitcast(dt.uint8), [T.P1c[:, 128 + 80 * o:208 + 80 * o].bitcast(dt.uint8) for o in at], "a1", "locA")
-    bcast(T.P1s[:, 48:128], [T.P1s[:, 128 + 80 * o:208 + 80 * o] for o in at], "a1", "locA")
-    a0 = ("a0", 2 * (N - 1) * NE_)
-    a1 = ("a1", 2 * (N - 1) * NE_)
-    locA = ("locA", 4 * NE_)
-    l_r2 = D("s", [locA], (T.TR[:, 0:1280], T.r2[:, :]))
-    l_w = D("s", [], (T.TW[:, :], T.w[:, :]))
-    i_3 = R("g", [], io(T.IT[:, 0:320], [[1, 320]], 0, 0), io(T.NT[:, 48:368], [[0, 4], [1, 80]], 0, 0))
+    bcast(u8("L0c", 106, 128), [u8("L0c", cq[s], cq[s] + 22) for s in far], mask(eng[0::2]), "ac", "locA")
+    bcast(T.L0s[:, 106:128], [T.L0s[:, cq[s]:cq[s] + 22] for s in far], mask(eng[1::2]), "asc", "locA")
+    ac = ("ac", (N - 1) * NE_ // 2)
+    asc = ("asc", (N - 1) * NE_ // 2)
+    locA = ("locA", NE_)
 
-    p_uc = R("v", [f_e, q_a], pickc("UR", 0, 128, "P0", 0, 32, T.OZ[:, 0:8]))
-    p_us = R("a", [f_e, q_a], picks("UR", 0, 128, "P0", 0, 32, T.OZ[:, 0:8]))
-    k4 = R("v", [k3],
-           ts(CP[:, 20:21], c1(0), 20.0 * rank - 48, c1(32), A.add, A.add),
-           ts(CP[:, 34:35], c1(0), 1.0 / 512, c1(33), A.mult, A.add))
-    q_e = R("v", [k3], *[qz("E", 128 * b, 128 * b + 128, T.TE[:, 3 - b:515 - b]) for b in range(4)])
-    m_h = R("t", [q_e, q_a], *[mm(T.PD[:, 512 * b:512 * b + 128], "E", 128 * b, "P0", 0, 128, True, True) for b in range(4)])
-    k4b = R("v", [k4],
-            ts(CP[:, 40:41], c1(20), -20.0 * rank, None, A.add),
-            ts(CP[:, 41:42], c1(20), 80.0 - 20.0 * rank, None, A.add))
-    cut = 80 - 20 * rank
-    k6 = R("v", [k3a],
-           ts(CP[:, 12:15], T.J[:, 0:12:4], c1(35), None, A.add),
-           ts(CP[:, 8:11], T.J[:, 0:12:4], c1(35), c1(11), A.add, A.add),
-           ts(CP[:, 16:19], T.J[:, 0:12:4], c1(35), c1(15), A.add, A.add),
-           ts(T.OX[:, 0:8:2], T.Z32[:, 0:4], c1(6), None, A.add),
-           ts(T.OX[:, 1:8:2], T.Z32[:, 0:4], c1(7), None, A.add))
-    k5 = R("v", [k4b], ts(T.TH0[:, 0:cut], T.J[:, 0:cut], c1(40), EPS, A.subtract, A.mult),
-           *([ts(T.TH0[:, cut:80], T.J[:, cut:80], c1(41), EPS, A.subtract, A.mult)] if rank else []))
-    seg = [(0, 64), (64, 84), (84, 104), (104, 128)]
-    k6a = R("a", [k3a],
-            act(T.GN[:, :], T.J[:, :], ID, bias=c1(37), scale=1.0 / 64),
-            act(T.TRI[:, :], T.J[:, 0:32], ID, bias=c1(22), scale=-1.0),
-            act(T.C115[:, :], T.J[:, 0:32], ID, bias=11.5, scale=0.0),
-            act(T.NT[:, 0:48], T.J[:, 0:48], ID, scale=0.0),
-            act(T.IT[:, 320:328], T.J[:, 0:8], ID, bias=-1.0, scale=0.0),
-            act(T.NR[:, 128:136], T.J[:, 0:8], ID, bias=-1.0, scale=0.0))
-    k7a = R("a", [k6a, k6],
-            act(CP[:, 42:45], CP[:, 8:11], ID, scale=-1.0), act(CP[:, 45:48], CP[:, 12:15], ID, scale=-1.0),
-            *[act(T.GTB[:, seg[o][0]:seg[o][1]], T.GN[:, seg[o][0]:seg[o][1]], ID, bias=64.0 * own_q[o] - (44 + 20 * o) / 64)
-              for o in range(N)])
-    c_h = R("a", [m_h], act(T.DH[:, 0:4], T.PD[:, 1:2048:512], AF.Copy))
-    k7 = R("v", [i_2],
-           ts(T.CM[:, :], T.CMI[:, :], c1(36), EPS, A.subtract, A.mult),
-           ms(T.TR[:, 1280:1288], 0.0), ms(T.TX1[:, 512:520], 0.0),
-           *[ms(T.QT[:, seg[o][0]:seg[o][1]], EPS * 128 * own_q[o]) for o in range(N)])
+    def xrow(a, col, m, u1, u0, last, base):
+        m1, m0 = m >> 1, m & 1
+        return io(ZB[quad(a), col:col + 12], [[u1 * (1 - 2 * m1), 2], [u0 * (1 - 2 * m0), 2], [last, 3]],
+                  base + u1 * m1 + u0 * m0, 0)
+    i_x = R("g", [f_x, i_p, i_j, i_z, i_o],
+            *([xrow(a, 0, a, 3, 16, 1, 0) for a in range(4)] +
+              [xrow(a, 32, a ^ rank, 32, 64, 0, 31) for a in range(4)] +
+              [io(T.TQ[quad(s), 4:8], [[1, 4]], -peer[s], 0) for s in range(4)]))
+    i_t = R("g", [i_x], io(T.IT[:, :], [[1, 336]], 0, 0))
+    i_b = R("g", [], io(T.NT[:, :], [[0, 4], [1, 84]], -4, 0),
+            io(T.BI[:, 0:18], [[0, 6], [4, 3]], 0, 0), io(T.BI[:, 24:42], [[3, 6], [257, 3]], 0, 0))
 
-    m_r0 = R("t", [a0, p_uc, p_us], mm(T.PA[:, 0:128], "UR", 0, "P0", 60, 128, True, True),
-             mm(T.PB[:, 0:128], "P0", 60, "P0", 0, 128, True, True))
-    x = d0 = R("v", [m_r0], ts(T.D0[:, :], T.PA[:, 48:128], T.PB[:, 0:1], None, A.subtract))
-    x = R("v", [x, k5], tt(T.C0[:, :], T.D0[:, :], T.TH0[:, :], A.is_gt))
-    x = R("v", [x], red(COL[:, 0:1], T.C0[:, :]))
-    x = R("v", [x], *spread(T.Z0, T.Z32, (COL, 0), (CP, 34)))
-    kr0 = R("v", [x], *turn(T.KR0, T.Z0))
-    sa = R("a", [kr0], act(T.S0[:, 128:256], T.KR0[:, :], AF.Abs, bias=c1(21)))
-    x = R("v", [kr0], ts(T.S0[:, 0:128], T.KR0[:, :], c1(6), None, A.subtract))
-    f0 = R("v", [x], rmin(COL[:, 1:2], T.S0[:, 0:128]))
-    f1 = R("v", [sa], rmin(COL[:, 2:3], T.S0[:, 128:256]))
-    o_v = R("v", [f0, f1], *[ts(T.OV[:, h:8:2], CP[:, 24:28], COL[:, 1 + h:2 + h], 512.0, A.add, A.mult) for h in range(2)])
-    o_e = R("v", [], *[ts(T.OE[:, h:8:2], CP[:, 28:32], COL[:, 1 + h:2 + h], 2048.0, A.add, A.mult) for h in range(2)])
-    p_vc = R("v", [o_v, a0], pickc("V1", 0, 128, "P0", 64, 188, T.OV[:, 0:8]))
-    m1 = R("a", [o_v, k7, k7a], ga(T.G64[:, 0:32], T.GTB[:, :], T.OV[:, 0:2]), ga(T.G64[:, 32:64], T.QT[:, :], T.OV[:, 0:2]))
-    p_vs = R("a", [a0], picks("V1", 0, 128, "P0", 64, 188, T.OV[:, 0:8]))
-    p_es = R("a", [o_e, a1, q_b], picks("E1", 0, 128, "P1", 0, 368, T.OE[:, 0:8]))
-    m2 = R("v", [m1], tr(T.GT[:, :], T.G64[:, :]))
-    qc = T.GT[:, 32:33]
-    m3 = R("v", [m2], ts(T.NE[:, :], T.G64[:, 32:64], qc, HUGE, A.not_equal, A.mult),
-           ts(T.D32[:, :], T.G64[:, 32:64], qc, None, A.subtract))
-    p_ec = R("v", [o_e, a1, q_b], pickc("E1", 0, 128, "P1", 0, 368, T.OE[:, 0:8]))
-    wait("t", [p_vc, p_vs, c_h])
+    k3 = R("v", [k2, i_j, f_e],
+           ts(T.TE[:, 3:515:4], J[:, :], c1(0), None, A.is_equal),
+           ts(T.OR[:, :], J[:, 12:44:4], c1(4), 31.0, A.add, A.min),
+           ts(T.DJ[:, :], J[:, 0:48], c1(3), None, A.subtract))
+    k3a = R("a", [k2, i_j],
+            act(CP[:, 7:8], c1(3), AF.Relu, bias=-86.0, scale=4.0),
+            act(CP[:, 8:9], c1(3), AF.Relu, bias=12.0, scale=-8.0),
+            act(CP[:, 9:10], c1(5), ID, bias=120.0),
+            act(CP[:, 12:13], c1(2), ID, bias=c1(5), scale=-336.0),
+            act(CP[:, 13:14], c1(2), ID, bias=c1(5), scale=4.0),
+            act(CP[:, 14:15], c1(4), ID, bias=0.5),
+            act(CP[:, 15:16], c1(1), ID, bias=16.0 / 1024, scale=1.0 / 1024),
+            fill(T.W0[:, :], 96, -4.0), fill(T.WS[:, 0:88], 88, 1.0), fill(T.WS[:, 88:89], 1, 1.0 / 32))
+    rr_s = R("a", [k3, q_a], picks("RR", 0, 128, "L0", 96, 128, T.OR[:, 0:8]))
+    q_r1 = R("v", [l_r1, f_b], qz("R1", 0, 128, T.TB[:, :]))
+    rr_c = R("v", [k3, q_a], pickc("RR", 0, 128, "L0", 96, 128, T.OR[:, 0:8]))
+    q_e = [R("v", [k3], qz("E", 128 * b, 128 * b + 128, T.TE[:, 3 - b:515 - b])) for b in range(4)]
+    wait("t", [rr_c, rr_s, q_r1])
+    m_s = []
     for b in range(4):
-        mm(T.PD[:, 512 * b:512 * b + 128], "E", 128 * b, "V1", 0, 128, True, False)()
-    m_e = [R("t", [p_ec, p_es], mm(T.PD[:, 512 * b:512 * b + 128], "E", 128 * b, "E1", 0, 128, False, True)) for b in range(4)]
-    m4 = R("v", [m3, k6a], tt(T.SAME[:, :], T.NE[:, :], T.TRI[:, :], A.is_lt))
-    m5 = R("v", [m4], red(COL[:, 3:4], T.SAME[:, :]))
-    m6 = R("v", [m5], ts(T.INVB[:, :], T.C115[:, :], COL[:, 3:4], HUGE, A.is_lt, A.mult))
-    cs = []
-    for b in range(2):
-        cs.append(R("a", [m_e[b], c_h], act(T.TX1[:, b:512:4], T.PD[:, 512 * b:512 * b + 128], ID, bias=T.DH[:, b:b + 1])))
-    m7 = R("v", [m6], tr(T.INVR[:, :], T.INVB[:, :]), tt(T.BASE[:, :], T.GT[:, 0:32], T.INVB[:, :], A.add))
-    cs.append(R("v", [m_e[3], m_e[2], c_h], *[ts(T.TX1[:, b:512:4], T.PD[:, 512 * b:512 * b + 128], T.DH[:, b:b + 1], None, A.add)
-                                              for b in (2, 3)]))
-    m8 = R("v", [m7], tt(T.W32[:, :], T.D32[:, :], T.INVR[:, :], A.add))
-    q_x1 = R("v", cs, qz("X1", 0, 130, T.TX1[:, :]))
-    m_r1 = R("t", [q_x1, d0], mm(T.PA[:, 0:128], "UR", 0, "X1", 0, 128, True, True),
-             mm(T.PB[:, 0:128], "X1", 0, "P0", 0, 128, True, True))
-    sm0 = R("a", [m3, k6], lambda: S.activation(T.JK[:, :], T.D32[:, :].indirect(T.OX[:, 0:8]), AF.Abs, scale=2.0 ** 68))
-    sm = R("a", [sm0], act(T.SM[:, :], T.JK[:, :], AF.Relu, bias=1.0, scale=-1.0))
-    m9 = R("v", [m8, k6], tt(T.THA[:, :], T.W32[:, :].indirect(T.OX[:, 0:8]), T.CM[:, :], A.add))
+        wait("t", [q_e[b]])
+        mm(T.PD[:, 512 * b:512 * b + 128], "E", 128 * b, "RR", 0, 128, True, False)()
+        m_s.append(R("t", [], mm(T.PD[:, 512 * b:512 * b + 128], "E", 128 * b, "R1", 0, 128, False, True)))
+    q_r4 = R("v", [q_a, f_b, i_z], qz("R4", 0, 234, T.TA[:, :]), cp(T.OZ[:, :], T.BI[:, 48:56]))
+    k4a = R("a", [k3a],
+            act(T.C0[:, 88:89], c1(8), ID, bias=c1(7), scale=-1.0),
+            act(CP[:, 11:12], c1(2), ID, bias=c1(9), scale=84.0),
+            act(CP[:, 16:17], c1(12), ID, bias=-16.0),
+            act(CP[:, 17:18], c1(14), ID, bias=c1(15)),
+            *([act(T.TH0[:, 22 * s + 2:22 * s + 22], T.DJ[:, 2:22], ID, bias=20.0 * (peer[s] - rank) * EPS, scale=EPS) for s in range(4)] +
+              [fill(T.TH0[:, 0:88:22], 4, HUGE), fill(T.TH0[:, 1:88:22], 4, HUGE)] +
+              [fill(T.TX1[:, 336 * s:336 * s + 16], 16, 0.0) for s in range(4)]))
+    c_s = R("a", m_s, *[act(T.S1[:, 80 * b:80 * b + 80], T.PD[:, 512 * b:512 * b + 80], AF.Copy) for b in range(4)])
+    f_p = R("v", [], ms(T.PT[:, :], 0.0))
+    z_c = R("v", [q_r4, f_b], pickc("LP2", 0, 16, "R4", 0, 32, T.OL[:, 4:5]))
+    z_s = R("a", [q_r4, f_b], picks("LP2", 0, 16, "R4", 0, 32, T.OL[:, 4:5]))
+    k7a = R("a", [f_p, k4a], fill(T.W0[:, 31:96:32], 3, c1(11)), *(
+            [fill(T.PT[:, k:336:84], 4, HUGE) for k in range(4)] +
+            [act(T.THS[:, 48 * h:48 * h + 48], T.DJ[:, :], ID, bias=(0.5 - 32 * h) * EPS, scale=EPS) for h in range(2)]))
+    q_r2 = R("v", [l_r2], qz("R2", 0, 320, T.TR[:, :]))
+    k5 = R("v", [i_x, k3a], cp(ZB[:, 16:28], ZB[:, 0:12]), cp(ZB[:, 48:60], ZB[:, 32:44]), cp(T.OX[:, 6:7], c1(13)))
+    k7 = R("v", [k5], tr(T.XT[:, :], ZB[:, 0:64]))
+    k8 = R("v", [k7], cp(T.OX[:, 0:8:4], T.XT[:, 0:64:32]))
 
-    d1 = R("v", [m_r1], ts(T.D1[:, :], T.PA[:, 0:128], T.PB[:, 0:1], None, A.subtract))
-    ca = R("v", [d1, m9], tt(T.CA[:, :], T.D1[:, :], T.THA[:, :], A.is_gt))
-    ra = R("a", [ca, sm], lambda: S.activation(T.JK[:, :], T.CA[:, :], AF.Copy, accum_out=COL[:, 4:5]))
-    cb = R("v", [ca, sm], tt(T.CB[:, :], T.CA[:, :], T.SM[:, :], A.mult))
-    tf = R("a", [ra], act(COL[:, 6:7], COL[:, 4:5], AF.Relu, bias=-31.0 * 1024, scale=1024.0))
-    rb = R("v", [cb], red(COL[:, 5:6], T.CB[:, :]))
-    x = R("v", [rb, tf], *spread(T.Z1, T.BASE, (COL, 5), (COL, 6)))
-    kr1 = R("v", [x], *turn(T.KR1, T.Z1))
-    sb = [R("a", [kr1], act(T.S1[:, 128 * j:128 * j + 128], T.KR1[:, :], AF.Abs, bias=c1(42 + j))) for j in (1, 2)]
-    x = R("v", [kr1], ts(T.S1[:, 0:128], T.KR1[:, :], c1(8), None, A.subtract))
-    r_e = [R("v", [d], rmin(T.RES[:, j:j + 1], T.S1[:, 128 * j:128 * j + 128])) for j, d in enumerate([x] + sb)]
+    ur_c = R("v", [ac, asc, q_r4], pickc("UR", 0, 128, "L0", 96, 194, T.OZ[:, 0:8]))
+    ur_s = R("a", [ac, asc, q_r4], picks("UR", 0, 128, "L0", 96, 194, T.OZ[:, 0:8]))
+    uo_c = R("v", [], pickc("UO", 0, 128, "L0", 96, 128, T.OU[:, 0:8]))
+    wait("t", [ac, asc, q_r4])
+    for s in range(3):
+        mm(T.PB[:, 0:128], "R4", 106 - 32 * s, "L0", 22 * s, 128, s == 0, False)()
+    m_c = R("t", [], mm(T.PB[:, 0:128], "R4", 10, "L0", 66, 128, False, True))
+    m_r = R("t", [ur_c, ur_s], mm(T.PA[:, 0:128], "UR", 0, "L0", 66, 128, True, True))
+    m_h = [R("t", [c_s], mm(T.PD[:, 512 * b:512 * b + 128], "E", 128 * b, "L0", 66, 128, True, True)) for b in range(4)]
+    c_h = [R("a", [m_h[b]], act(DH[:, 4 * b:4 * b + 4], T.PD[:, 512 * b + 41:512 * b + 108:22], AF.Copy)) for b in range(4)]
+    x1 = [R("a", c_h + [c_s],
+            *[act(T.TX1[:, 336 * s + 16 + b:336 * s + 336:4], T.S1[:, 80 * b:80 * b + 80], ID,
+                  bias=DH[:, 4 * b + s:4 * b + s + 1]) for s in ss for b in range(4)]) for ss in ((0, 1), (2, 3))]
+    x = d0 = R("v", [m_r, m_c], ts(T.D0[:, :], T.PA[:, 40:128], T.PB[:, 106:107], None, A.subtract))
+    x = R("v", [x, k4a], tt(T.C0[:, 0:88], T.D0[:, :], T.TH0[:, :], A.is_gt))
+    x = R("v", [x, k3a], scan(T.SA[:, 0:89], T.WS[:, 0:89], T.C0[:, 0:89]))
+    x = R("v", [x, i_o], ts(T.M0[:, :], T.IO[:, :, :], T.SA[:, 21:22], T.SA[:, 88:89], A.is_equal, A.is_le))
+    x = R("v", [x], tr(T.MT0[:, :], T.M0[:, :]))
+    x = R("v", [x, k7a], scan(T.SC0[:, :], T.MT0[:, :], T.W0[:, :]))
+    x = R("v", [x, f_x], cp(ZB[:, G0:G0 + 3], T.SC0[:, 31:96:32]), cp(ZB[LO, G0 + 3:G0 + 6], T.SC0[HI, 31:96:32]),
+          cp(ZB[HI, G0 + 3:G0 + 6], T.SC0[LO, 31:96:32]))
+    o_l = R("v", [z_c, z_s], cp(T.OL[:, 0:3], T.SC0[:, 31:96:32]))
+    q_x1a = R("v", [x1[0]], qz("X1", 0, 168, T.TX1[:, 0:672]))
+    n_p = R("a", [o_l, k7a, i_t], ga(T.NP[:, 0:64], T.IT[:, :], T.OL[:, 0:4]), ga(T.NP[:, 64:128], T.PT[:, :], T.OL[:, 0:4]))
+    x = R("v", [x], *[cp(ZB[quad(a ^ 1), G0 + 16:G0 + 22], ZB[quad(a), G0:G0 + 6]) for a in range(4)])
+    q_x1b = R("v", [x1[1]], qz("X1", 168, 336, T.TX1[:, 672:1344]))
+    o_0 = R("v", [x, k8], cp(T.O0[:, :], ZB[:, G0:G0 + 32].indirect(T.OX[:, 0:1])))
+    p1c = R("v", [o_0, q_x1a, q_x1b], pickc("P1", 0, 208, "X1", 0, 336, T.O0[:, 0:13]))
+    p1s = R("a", [o_0, q_x1a, q_x1b], picks("P1", 0, 208, "X1", 0, 336, T.O0[:, 0:13]))
+    npt = R("v", [n_p], tr(T.NPT[:, :], T.NP[:, :]))
+    th1 = R("v", [], *[tt(T.TH1[:, 48 * h:48 * h + 48], T.NP[:, 64:112], T.THS[:, 48 * h:48 * h + 48], A.add) for h in range(2)])
+    uo_s = R("a", [], picks("UO", 0, 128, "L0", 96, 128, T.OU[:, 0:8]))
 
-    wait("g", r_e)
-    bcast(T.RES[:, 0:3], [T.LAND[:, 3 * o:3 * o + 3] for o in at], "lb", "locB")
-    lb = ("lb", (N - 1) * NE_)
+    wait("g", [o_0])
+    deal([T.O0[:, 3 * s:3 * s + 3] for s in far], T.LL0[:, 3 * rank:3 * rank + 3], m_b, "l0")
+    wait("g", [p1c])
+    deal([u8("P1c", 48 * s, 48 * s + 48) for s in far], u8("LP1c", 48 * rank, 48 * rank + 48), m_a, "p1")
+    wait("g", [p1s])
+    deal([T.P1s[:, 48 * s:48 * s + 48] for s in far], T.LP1s[:, 48 * rank:48 * rank + 48], m_b, "p1")
+    h_l0 = D("s", [o_0], (T.LL0[:, 3 * rank:3 * rank + 3], T.O0[:, 0:3]))
+    h_p1 = D("s", [p1c, p1s], (u8("LP1c", 48 * rank, 48 * rank + 48), u8("P1c", 0, 48)),
+             (T.LP1s[:, 48 * rank:48 * rank + 48], T.P1s[:, 0:48]))
+    l0 = ("l0", NE_)
+    p1 = ("p1", 2 * NE_)
 
-    q_r2 = R("v", [l_r2], qz("R2", 0, 322, T.TR[:, :]))
-    n_r = R("a", [i_3], ga(T.NR[:, 0:128], T.NT[:, :], T.OE[:, 0:8]))
-    b0 = R("v", r_e, ts(T.BC0[:, :], T.GT[:, 32:64], 2.0 ** 74, c1(39), A.mult, A.add),
-           ts(COL[:, 7:8], COL[:, 3:4], c1(38), None, A.add),
-           ts(T.RU[:, 0, 0:3], T.RES[:, 0:3], 1024.0, 320.0, A.mult, A.min))
-    x = R("v", [b0], tt(T.BC[:, :], T.BC0[:, :], T.INVB[:, :], A.add),
-          ts(T.ZP[:, :], T.GT[:, 32:64], 2.0 ** 74, COL[:, 7:8], A.mult, A.add))
-    x = R("v", [x], tr(T.KRP[:, :], T.ZP[:, :]), *spread(T.Z2, T.BC, (COL, 5), (COL, 6)))
-    kr2 = R("v", [x], *(turn(T.KR2, T.Z2) +
-                        [ts(T.SP[:, 32 * j:32 * j + 32], T.KRP[:, :], c1(16 + j), None, A.subtract) for j in range(3)]))
-    xs = R("a", [kr2], *[act(T.S2[:, 128 * j:128 * j + 128], T.KR2[:, :], AF.Abs, bias=c1(45 + j)) for j in range(3)])
-
-    x = R("v", [lb], *[ts(T.OW[32 * a:32 * a + 32, 0:9], T.LAND[32 * rank:32 * rank + 32, 0:9], 1024.0, 320.0, A.mult, A.min)
-                       for a in range(4)])
-    s_c = R("v", [x, q_r2], pickc("SN", 0, 144, "R2", 0, 322, T.OW[:, 0:9]))
-    s_s = R("a", [x, q_r2], picks("SN", 0, 144, "R2", 0, 322, T.OW[:, 0:9]))
-    u = NE_ // 4
-    mc = [mask(eng[0:u]), mask(eng[u:2 * u]), mask(eng[2 * u:])]
-    msk = [mask(eng[0:2 * u]), mask(eng[2 * u:3 * u]), mask(eng[3 * u:])]
-    wait("g", [s_c])
-    g.remote_dma_fused([RemoteDMATransfer(dst_ids=[ids[s]], dma_engine_mask=mc[s], remote_sem=T.sem.ce,
-                                          src=T.SNc[:, 48 * s:48 * s + 48].bitcast(dt.uint8),
-                                          dst=T.E2c[:, 48 * rank:48 * rank + 48].bitcast(dt.uint8)) for s in range(N - 1)],
-                       local_sem=T.sem.locB)
-    wait("g", [s_s])
-    g.remote_dma_fused([RemoteDMATransfer(dst_ids=[ids[s]], dma_engine_mask=msk[s], remote_sem=T.sem.ce,
-                                          src=T.SNs[:, 48 * s:48 * s + 48],
-                                          dst=T.E2s[:, 48 * rank:48 * rank + 48]) for s in range(N - 1)],
-                       local_sem=T.sem.locB)
-    ce = ("ce", 2 * NE_)
-    locB = ("locB", 3 * NE_)
-
-    x = R("v", [xs], *([rmin(COL[:, 12 + j:13 + j], T.S2[:, 128 * j:128 * j + 128]) for j in range(3)] +
-                       [rmin(COL[:, 16 + j:17 + j], T.SP[:, 32 * j:32 * j + 32]) for j in range(3)]))
-    x = R("v", [x], ts(T.RU[:, 1, 0:3], COL[:, 12:15], 512.0, 128.0, A.mult, A.min),
-          ts(T.RU[:, 2, 0:3], COL[:, 16:19], 512.0, 128.0, A.mult, A.min))
-    ow = R("v", [b0], *[cp(T.OWN[32 * a:32 * a + 32, 0:3], T.RU[32 * rank:32 * rank + 32, 0, 0:3]) for a in range(4)])
-    fu = R("v", [x], *[cp(T.FULL[32 * a:32 * a + 32, :, 3 * q:3 * q + 3], T.RU[32 * q:32 * q + 32, :, 0:3])
-                       for q in range(N) for a in range(4)])
-    e2s = R("a", [ow], picks("E2", 48 * rank, 48, "R2", 0, 322, T.OWN[:, 0:3]))
-    n2 = R("a", [fu, i_3], ga(T.NM[:, 192:384], T.IT[:, :], T.FULL[:, 0, :]))
-    e2c = R("v", [ow], pickc("E2", 48 * rank, 48, "R2", 0, 322, T.OWN[:, 0:3]))
-    v2c = R("v", [fu], pickc("V2", 0, 192, "X1", 0, 130, T.FULL[:, 1, :]))
-    v2s = R("a", [q_x1], picks("V2", 0, 192, "X1", 0, 130, T.FULL[:, 1, :]))
-    o1s = R("a", [], picks("O1", 0, 192, "X1", 0, 130, T.FULL[:, 2, :]))
-    o1c = R("v", [], pickc("O1", 0, 192, "X1", 0, 130, T.FULL[:, 2, :]))
-    hm = R("v", [n2], *[ts(T.HM[:, 192 * b:192 * b + 192], T.NM[:, 192:384], -0.5, T.DH[:, b:b + 1], A.is_gt, A.mult)
-                        for b in range(4)])
+    m_1 = R("t", [p1c, p1s, d0], mm(T.PA[:, 0:208], "UR", 0, "P1", 0, 208, True, True))
+    zt = R("v", [m_1], *[tr(T.ZT[quad(s), :], T.PA[quad(s), 48 * s:48 * s + 64]) for s in range(4)])
+    x = R("v", [zt], tr(T.RA[:, :], T.ZT[:, :]))
+    msa = R("a", [zt], act(T.ML[:, 0:2], T.ZT[:, 0:64:32], AF.Copy))
+    k9a = R("a", [i_b, i_x], act(T.AB[:, 16:32], T.BI[:, 0:16], ID, bias=c1(14)),
+            act(T.AB[:, 0:16], T.BI[:, 24:40], ID, bias=c1(17), scale=1.0 / 64),
+            act(T.TQ[:, 0:4], T.TQ[:, 4:8], ID, scale=EPS),
+            fill(T.RS[:, :], 128, 1.0), fill(T.NR[:, 0:16], 16, -1.0), fill(T.KT[:, 0:16], 16, 0.0),
+            fill(T.KT[:, 16:112], 96, 1.0), fill(T.KT[:, 112:208], 96, 1.0),
+            *[fill(T.NT[:, k:336:84], 4, -1.0) for k in range(3)])
+    x = R("v", [x, npt], *[ts(T.D1[:, 48 * h:48 * h + 48], T.RA[:, 0:48], T.ZT[:, 32 * h:32 * h + 1],
+                              T.NPT[:, 64 + 32 * h:65 + 32 * h], A.subtract, A.add) for h in range(2)])
+    x = R("v", [x, th1], tt(T.C1[:, :], T.D1[:, :], T.TH1[:, :], A.is_ge))
+    rk = R("v", [x], *[red(T.ML[:, 2 + h:3 + h], T.C1[:, 48 * h:48 * h + 48]) for h in range(2)])
+    wait("g", [rk, msa])
+    bcast(T.ML[:, 0:4], [T.ML[:, 4 * s:4 * s + 4] for s in far], mask(eng), "ms", "locB")
+    msg = ("ms", (N - 1) * NE_)
+    x = R("v", [rk], *[ts(T.M1[:, :, 32 * h:32 * h + 32], T.IO[:, :, :], T.ML[:, 2 + h:3 + h], T.NPT[:, 32 * h:32 * h + 1],
+                          A.is_equal, A.mult) for h in range(2)])
+    x = R("v", [x], tr(T.MT1[:, :], T.M1[:, :, :]))
+    k10a = R("a", [k9a], fill(T.RS[:, 0:128:32], 4, 0.0),
+             *[act(T.TQ[quad(s), peer[s]:peer[s] + 1], J[quad(s), 0:1], ID, bias=HUGE, scale=0.0) for s in range(4)])
+    x = R("v", [x], *[red(ZB[:, G1 + c:G1 + c + 1], T.MT1[:, 64 * c:64 * c + 64]) for c in range(3)])
+    g1v = R("v", [x], cp(ZB[LO, G1 + 3:G1 + 6], ZB[HI, G1:G1 + 3]), cp(ZB[HI, G1 + 3:G1 + 6], ZB[LO, G1:G1 + 3]))
+    g1a = R("a", [x], *[act(ZB[o, G1 + c:G1 + c + 3], ZB[i, G1:G1 + 3], ID, bias=CP[i, 16:17], scale=4.0)
+                        for o, c, i in ((ALL, 8, ALL), (LO, 11, HI), (HI, 11, LO))])
+    g2v = R("v", [g1v, g1a], *[cp(ZB[quad(a ^ 1), G1 + 16:G1 + 30], ZB[quad(a), G1:G1 + 14]) for a in (0, 1)])
+    g2a = R("a", [g1v, g1a], *[act(ZB[quad(a ^ 1), G1 + 16:G1 + 30], ZB[quad(a), G1:G1 + 14], AF.Copy) for a in (2, 3)])
+    o_v = R("v", [g2v, g2a], cp(T.OV[:, :], ZB[:, G1:G1 + 32].indirect(T.OX[:, 0:1])))
+    o_e = R("v", [], cp(T.OE[:, :], ZB[:, G1 + 8:G1 + 32].indirect(T.OX[:, 0:1])))
+    v2c = R("v", [o_v], pickc("V2", 0, 192, "X1", 0, 336, T.OV[:, 0:12]))
+    v2s = R("a", [o_v], picks("V2", 0, 192, "X1", 0, 336, T.OV[:, 0:12]))
+    e2c = R("v", [o_e, q_r2], pickc("E2", 0, 192, "R2", 0, 320, T.OE[:, 0:12]))
+    e2s = R("a", [o_e, q_r2], picks("E2", 0, 192, "R2", 0, 320, T.OE[:, 0:12]))
+    wait("g", [o_e])
+    deal([T.OE[:, 3 * s:3 * s + 3] for s in far], T.LL1[:, 3 * rank:3 * rank + 3], m_b, "l1")
+    h_l1 = D("s", [o_e], (T.LL1[:, 3 * rank:3 * rank + 3], T.OE[:, 0:3]))
+    l1 = ("l1", NE_)
     q_w = R("v", [l_w], qz("W", 0, 128, T.TW[:, :]))
-    n1 = R("a", [n_r], ga(T.NM[:, 0:192], T.NR[:, :], T.FULL[:, 2, :]))
-    wait("t", [v2c, v2s] + cs)
+    pa1 = R("a", [l0, h_l0], ga(T.PA1[:, :], T.PT[:, :], T.LL0[:, 0:12]))
+    wait("t", [v2c, v2s] + c_h)
     for b in range(4):
         mm(T.PD[:, 512 * b:512 * b + 192], "E", 128 * b, "V2", 0, 192, True, False)()
-    m_y0 = R("t", [o1c, o1s, q_w], mm(T.PY[:, 0:192], "W", 0, "O1", 0, 192, True, True))
-    c_y0 = R("a", [m_y0], act(T.Y[:, 0:192], T.PY[:, 0:192], AF.Copy))
-    D("s", [n1, n2], (T.nm[:, :], T.NM[0:1, :]))
-    D("s", [c_y0, locB], (T.y[:, 0:192], T.Y[:, 0:192]))
-
-    m_e2 = [R("t", [ce, e2c, e2s], mm(T.PD[:, 512 * b:512 * b + 192], "E", 128 * b, "E2", 0, 192, False, True)) for b in range(4)]
-    name = newsem()
+    m_e = [R("t", [e2c, e2s], mm(T.PD[:, 512 * b:512 * b + 192], "E", 128 * b, "E2", 0, 192, False, True)) for b in range(4)]
+    m_a1 = R("t", [p1, h_p1, uo_c, uo_s, d0], mm(T.PB[:, 0:192], "UO", 0, "LP1", 0, 192, True, True))
+    m_y0 = R("t", [q_w], mm(T.PY[:, 0:192], "W", 0, "LP1", 0, 192, True, True))
+    cs = []
     for b in range(4):
-        wait("v", [hm, m_e2[b]])
-        tt(T.TX2[:, b:768:4], T.PD[:, 512 * b:512 * b + 192], T.HM[:, 192 * b:192 * b + 192], A.add)().then_inc(T.sem[name], 1)
-    total[name] = 4
-    q_x2 = R("v", [(name, 4)], qz("X2", 0, 192, T.TX2[:, :]))
-    m_y1 = R("t", [q_x2], mm(T.PY[:, 512:704], "W", 0, "X2", 0, 192, True, True))
-    c_y1 = R("v", [m_y1], cp(T.Y[:, 192:384], T.PY[:, 512:704]))
-    D("s", [q_x2], (T.oc[:, :], T.X2c[:, 0:192].bitcast(dt.uint8)),
-      *[(T.osc[4 * k:4 * k + 4, :], T.X2s[32 * k:32 * k + 4, 0:192]) for k in range(2)])
-    D("a", [q_x2], *[(T.osc[4 * k:4 * k + 4, :], T.X2s[32 * k:32 * k + 4, 0:192]) for k in range(2, 4)])
-    D("a", [c_y1], (T.y[:, 192:384], T.Y[:, 192:384]))
+        sides = [(T.TX2[:, 192 * s + b:192 * s + 192:4], T.PD[:, 512 * b + 48 * s:512 * b + 48 * s + 48],
+                  DH[:, 4 * b + s:4 * b + s + 1]) for s in range(4)]
+        if b % 2 == 0:
+            cs.append(R("a", [m_e[b]], *[act(o, i, ID, bias=h) for o, i, h in sides]))
+        else:
+            cs.append(R("v", [m_e[b]] + c_h, *[ts(o, i, h, None, A.add) for o, i, h in sides]))
+    q_x2 = R("v", cs, qz("X2", 0, 192, T.TX2[:, :]))
 
+    wait("g", [q_x2])
+    deal([u8("X2c", 48 * s, 48 * s + 48) for s in far], u8("LP2c", 16 + 48 * rank, 64 + 48 * rank), m_a, "p2c")
+    deal([T.X2s[:, 48 * s:48 * s + 48] for s in far], T.LP2s[:, 16 + 48 * rank:64 + 48 * rank], m_b, "p2s")
+    h_p2 = D("s", [q_x2], (u8("LP2c", 16 + 48 * rank, 64 + 48 * rank), u8("X2c", 0, 48)),
+             (T.LP2s[:, 16 + 48 * rank:64 + 48 * rank], T.X2s[:, 0:48]))
+    p2c = ("p2c", NE_)
+    p2s = ("p2s", NE_)
+    locB = ("locB", 7 * NE_)
+
+    cl = R("a", [msg, rk, msa, k7], ga(T.CL[:, :], T.ML[:, :], T.OX[:, 6:7]))
+    rm = R("v", [m_a1, pa1], tt(T.RM[:, :], T.PB[:, 0:192], T.PA1[:, :], A.subtract))
+    c_y0 = R("a", [m_y0], act(T.Y[:, 0:192], T.PY[:, 0:192], AF.Copy))
+    lim = R("a", [cl], act(T.LIM[:, 0:2], T.CL[:, 2:4], ID, bias=31.5, scale=-1.0))
+    fs = [R("v", [cl, rm, k10a], *[ts(T.F[:, 192 * h + 48 * q:192 * h + 48 * q + 48], T.RM[:, 48 * q:48 * q + 48], T.CL[:, h:h + 1],
+                                      T.TQ[:, q:q + 1], A.subtract, A.is_gt) for q in range(N)]) for h in range(2)]
+    o_a = R("a", [fs[0]], lambda: S.activation(T.JK[:, :], T.F[:, 0:192], AF.Copy, accum_out=T.O2[:, 0:1]))
+    o_b = R("v", [fs[1]], red(T.O2[:, 1:2], T.F[:, 192:384]))
+    x = R("v", [o_a, o_b, lim], tt(T.FG[:, 0:2], T.O2[:, 0:2], T.LIM[:, 0:2], A.is_lt))
+    n2 = R("a", [l1, h_l1], ga(T.NR[:, 16:208], T.IT[:, :], T.LL1[:, 0:12]))
+    x = R("v", [x], *[ts(T.Z2[o, c:c + 32], ZB[i, Z0:Z0 + 32], T.FG[i, 0:1], T.FG[i, 1:2], A.add, A.add)
+                      for o, c, i in ((ALL, 0, ALL), (LO, 32, HI), (HI, 32, LO))])
+    x = R("v", [x], tr(T.KR[:, 0:64], T.Z2[:, :]), *[tr(T.KR[quad(a), 64:128], T.Z2[quad(a ^ 1), :]) for a in range(4)])
+    n1 = R("a", [], ga(T.NM[:, 0:192], T.NT[:, :], T.LL0[:, 0:12]))
+    x = cnt = R("v", [x], scan(T.SCN[:, :], T.RS[:, :], T.KR[:, :]))
+    x = R("v", [x], tt(T.FA[:, :], T.SCN[:, :].indirect(T.OX[:, 4:5]), T.AB[:, 0:16], A.min))
+    x = R("v", [x], tt(T.FB[:, :], T.FA[:, :], T.AB[:, 16:32], A.subtract))
+    fl = R("v", [x], ts(T.FL[:, :], T.FB[:, :], 1024.0, None, A.mult))
+    D("s", [c_y0, cnt], (T.y[:, 0:192], T.Y[:, 0:192]))
+
+    mk = R("a", [fl], ga(T.MK[:, :], T.KT[:, :], T.FL[:, 0:12]))
+    xfc = R("v", [fl, p2c, h_p2], pickc("XF", 0, 192, "LP2", 0, 208, T.FL[:, 0:12]))
+    m_y1 = R("t", [p2c, p2s, h_p2], mm(T.PY[:, 512:704], "W", 0, "LP2", 16, 192, True, True))
+    xfs = R("a", [fl, p2s, h_p2], picks("XF", 0, 192, "LP2", 0, 208, T.FL[:, 0:12]))
+    c_y1 = R("v", [m_y1, mk], tt(T.Y[:, 192:384], T.PY[:, 512:704], T.MK[:, :], A.mult))
+    n3 = R("v", [n2], cp(T.NM[:, 192:384], T.NR[:, :].indirect(T.FL[:, 0:12])))
+    D("s", [xfc], (T.oc[:, :], u8("XFc", 0, 192)))
+    D("s", [c_y1], (T.y[:, 192:384], T.Y[:, 192:384]))
+    D("a", [xfs], *[(T.osc[4 * k:4 * k + 4, :], T.XFs[32 * k:32 * k + 4, :]) for k in range(4)])
+    D("s", [n1, n3], (T.nm[:, :], T.NM[0:1, :]))
+
+    wait("g", [locA, locB])
     for name in total:
         if max(known[q].get(name, 0) for q in known) < total[name]:
             wait("g", [(name, total[name])])

from concourse.bass import DstId, RemoteDMATransfer
from concourse.mybir import dt, AluOpType, AxisListType, ActivationFunctionType

FP8 = "float8_e4m3fn_x4"
SCRATCH = {}
for _n, _w in (("L0", 194), ("R4", 234), ("UR", 128), ("UO", 128), ("E", 512), ("RR", 128), ("R1", 128), ("R2", 320),
               ("X1", 336), ("P1", 208), ("LP1", 192), ("V2", 192), ("E2", 192), ("X2", 192), ("LP2", 208),
               ("XF", 192), ("W", 128)):
    SCRATCH[_n + "c"] = ("sbuf", [128, _w], FP8)
    SCRATCH[_n + "s"] = ("sbuf", [128, _w], "uint8")
for _n, _w in (("TA", 936), ("TB", 512), ("TR", 1280), ("TW", 512), ("TE", 520), ("TX1", 1344), ("TX2", 768)):
    SCRATCH[_n] = ("sbuf", [128, _w], "bfloat16")
for _n, _w in (("J", 128), ("CP", 32), ("ZB", 160), ("DJ", 48), ("TH0", 88), ("THS", 96), ("XT", 64),
               ("BI", 64), ("AB", 32), ("TQ", 8), ("W0", 96), ("WS", 96), ("RS", 128), ("IT", 336), ("NT", 336),
               ("PT", 336), ("KT", 208), ("S1", 320), ("DH", 16), ("D0", 88), ("C0", 96), ("SA", 96), ("M0", 96), ("MT0", 96),
               ("SC0", 96), ("NP", 128), ("NPT", 128), ("TH1", 96), ("ZT", 64), ("RA", 64), ("D1", 96),
               ("C1", 96), ("MT1", 192), ("ML", 16), ("CL", 16), ("LIM", 8), ("PA1", 192), ("RM", 192),
               ("F", 384), ("JK", 192), ("O2", 8), ("FG", 8), ("Z2", 64), ("KR", 128), ("SCN", 128), ("FA", 16), ("FB", 16),
               ("NR", 208), ("MK", 192), ("NM", 384), ("Y", 384)):
    SCRATCH[_n] = ("sbuf", [128, _w], "float32")
SCRATCH["IO"] = ("sbuf", [128, 3, 32], "float32")
SCRATCH["M1"] = ("sbuf", [128, 3, 64], "float32")
SCRATCH["CI"] = ("sbuf", [128, 8], "int32")
for _n, _w in (("OZ", 8), ("OU", 8), ("OR", 8), ("OX", 8), ("OL", 8), ("O0", 16), ("OV", 16), ("OE", 16), ("FL", 16),
               ("LL0", 16), ("LL1", 16)):
    SCRATCH[_n] = ("sbuf", [128, _w], "uint16")
SCRATCH["PA"] = ("psum", [128, 512], "float32")
SCRATCH["PB"] = ("psum", [128, 512], "float32")
SCRATCH["PD"] = ("psum", [128, 2048], "float32")
SCRATCH["PY"] = ("psum", [128, 1024], "float32")

NPOOL = 138
SEMAPHORES = ["ac", "asc", "l0", "p1", "ms", "l1", "p2c", "p2s", "locA", "locB"] + ["s%d" % _i for _i in range(NPOOL)]

EPS = 2.0 ** -75
HUGE = 1e29


def rank_program(g, core, T, topo):
    rank = T.rank_of(core)
    if rank is None:
        return
    N = len(T.cores)
    A = AluOpType
    AF = ActivationFunctionType
    V, S, TE_, SY = g.vector, g.scalar, g.tensor, g.sync
    Q = {"g": g, "v": V, "a": S, "t": TE_, "s": SY}
    known = {k: {} for k in Q}
    total = {}
    home = {}
    fresh = [0]

    def wait(q, deps):
        for d in deps:
            if d is None:
                continue
            name, cnt = d
            if known[q].get(name, 0) < cnt:
                Q[q].wait_ge(T.sem[name], cnt)
                known[q][name] = cnt

    def R(q, deps, *fns, inc=1):
        wait(q, deps)
        name = None
        if inc == 1:
            for n in total:
                if home[n] == q and known[q].get(n, 0) == total[n]:
                    name = n
                    break
        if name is None:
            name = "s%d" % fresh[0]
            fresh[0] += 1
            total[name] = 0
            home[name] = q if inc == 1 else None
        for fn in fns:
            fn().then_inc(T.sem[name], inc)
        total[name] += inc * len(fns)
        return (name, total[name])

    def D(q, deps, *pairs):
        return R(q, deps, *[(lambda o=o, i=i: Q[q].dma_start(o, i)) for o, i in pairs], inc=16)

    def ts(out, in0, s1, s2, op0, op1=None):
        if op1 is None:
            return lambda: V.tensor_scalar(out, in0, s1, None, op0)
        return lambda: V.tensor_scalar(out, in0, s1, s2, op0, op1)

    def tt(out, a, b, op):
        return lambda: V.tensor_tensor(out, a, b, op)

    def cp(out, a):
        return lambda: V.tensor_copy(out, a)

    def ms(out, c):
        return lambda: V.memset(out, c)

    def red(out, a):
        return lambda: V.tensor_reduce(out, a, AxisListType.X, A.add)

    def scan(out, d0, d1):
        return lambda: V.tensor_tensor_scan(out, d0, d1, 0.0, A.mult, A.add)

    def tr(out, a):
        return lambda: V.transpose(out, a)

    def act(out, a, func, bias=0.0, scale=1.0):
        return lambda: S.activation(out, a, func, bias=bias, scale=scale)

    def qz(n, a, b, tile):
        return lambda: V.quantize_mx(T[n + "c"][:, a:b], T[n + "s"][:, a:b], tile)

    def mm(out, w, wa, x, xa, n, start, stop):
        return lambda: TE_.matmul_mx(out, T[w + "c"][:, wa:wa + 128], T[w + "s"][:, wa:wa + 128],
                                     T[x + "c"][:, xa:xa + n], T[x + "s"][:, xa:xa + n], start, stop)

    def pickc(o, oa, n, w, wa, wb, off):
        return lambda: V.tensor_copy(T[o + "c"][:, oa:oa + n].bitcast(dt.uint32),
                                     T[w + "c"][:, wa:wb].bitcast(dt.uint32).indirect(off))

    def picks(o, oa, n, w, wa, wb, off):
        return lambda: S.activation(T[o + "s"][:, oa:oa + n], T[w + "s"][:, wa:wb].indirect(off), AF.Copy)

    def ga(out, win, off):
        return lambda: S.activation(out, win.indirect(off), AF.Copy)

    def io(out, pat, base, cm):
        return lambda: g.iota(out, pat, base, cm, allow_small_or_imprecise_dtypes=True)

    def u8(n, a, b):
        return T[n][:, a:b].bitcast(dt.uint8)

    def quad(a):
        return slice(32 * a, 32 * a + 32)
    LO, HI, ALL = slice(0, 64), slice(64, 128), slice(0, 128)

    peer = [rank ^ s for s in range(N)]
    far = list(range(1, N))
    ids = []
    eng = None
    for s in far:
        rid, pid, _se = topo.addr(T.cores[peer[s]])
        ids.append(DstId(rid=rid, pnc=pid))
        e = topo.engines(core, T.cores[peer[s]])
        eng = e if eng is None else [x for x in eng if x in e]

    def mask(es):
        m = 0
        for x in es:
            m |= 1 << x
        return m
    NE_ = len(eng)
    u = NE_ // 4
    m_a = [mask(eng[0:u]), mask(eng[u:2 * u]), mask(eng[2 * u:])]
    m_b = [mask(eng[0:2 * u]), mask(eng[2 * u:3 * u]), mask(eng[3 * u:])]

    def bcast(src, dsts, m, sem, loc):
        g.remote_dma_fused([RemoteDMATransfer(dst_ids=ids, dma_engine_mask=m, remote_sem=T.sem[sem],
                                              srcs=[src], dsts=dsts)], local_sem=T.sem[loc])

    def deal(srcs, dst, masks, sem):
        g.remote_dma_fused([RemoteDMATransfer(dst_ids=[ids[s]], dma_engine_mask=masks[s], remote_sem=T.sem[sem],
                                              src=srcs[s], dst=dst) for s in range(N - 1)], local_sem=T.sem.locB)

    CP, J, DH, ZB = T.CP, T.J, T.DH, T.ZB
    ID = AF.Identity
    cq = [106 + 22 * s for s in range(N)]
    G0, G1, Z0 = 64, 96, 128

    def c1(i):
        return CP[:, i:i + 1]

    def fill(out, n, c):
        return act(out, J[:, 0:n], ID, bias=c, scale=0.0)

    l_r0 = D("s", [], (T.TA[:, 432:512], T.r0[:, :]))
    l_u = D("a", [], (T.TA[:, 424:432], T.u[:, 0:8]))
    l_r1 = D("s", [], (T.TB[:, 0:320], T.r1[:, :]))
    l_r2 = D("s", [], (T.TR[:, :], T.r2[:, :]))
    l_w = D("s", [], (T.TW[:, :], T.w[:, :]))
    i_p = R("g", [], lambda: g.iota(T.CI[:, 0:1], [[1, 1]], 0, 1))
    i_j = R("g", [], io(J[:, :], [[1, 128]], 0, 0))
    f_a = R("v", [], ms(T.TA[:, 0:424], 0.0))
    f_x = R("v", [], ms(ZB[:, :], 0.0))
    k1 = R("v", [i_p],
           ts(T.CI[:, 1:2], T.CI[:, 0:1], 15, None, A.bitwise_and),
           ts(T.CI[:, 2:3], T.CI[:, 0:1], 5, None, A.logical_shift_right),
           ts(T.CI[:, 3:4], T.CI[:, 0:1], 31, None, A.bitwise_and),
           ts(T.CI[:, 4:5], T.CI[:, 0:1], 15, 2, A.bitwise_and, A.logical_shift_right),
           ts(T.CI[:, 5:6], T.CI[:, 0:1], 3, None, A.bitwise_and))
    f_e = R("v", [], ms(T.TE[:, :], 0.0))
    k2 = R("v", [k1], cp(CP[:, 0:6], T.CI[:, 0:6]))
    f_b = R("v", [], ms(T.TA[:, 512:936], 0.0), ms(T.TB[:, 320:512], 0.0), ms(T.OU[:, :], 10), ms(T.OL[:, :], 0))
    i_z = R("g", [], io(T.BI[:, 48:56], [[22, 4], [0, 2]], 10, 0))
    i_o = R("g", [], *[io(T.IO[:, c, :], [[0, 2], [1, 4], [0, 4]], 4 * c, 0) for c in range(3)])
    q_a = R("v", [l_r0, l_u, f_a], qz("L0", 0, 128, T.TA[:, 0:512]))

    wait("g", [q_a])
    bcast(u8("L0c", 106, 128), [u8("L0c", cq[s], cq[s] + 22) for s in far], mask(eng[0::2]), "ac", "locA")
    bcast(T.L0s[:, 106:128], [T.L0s[:, cq[s]:cq[s] + 22] for s in far], mask(eng[1::2]), "asc", "locA")
    ac = ("ac", (N - 1) * NE_ // 2)
    asc = ("asc", (N - 1) * NE_ // 2)
    locA = ("locA", NE_)

    def xrow(a, col, m, u1, u0, last, base):
        m1, m0 = m >> 1, m & 1
        return io(ZB[quad(a), col:col + 12], [[u1 * (1 - 2 * m1), 2], [u0 * (1 - 2 * m0), 2], [last, 3]],
                  base + u1 * m1 + u0 * m0, 0)
    i_x = R("g", [f_x, i_p, i_j, i_z, i_o],
            *([xrow(a, 0, a, 3, 16, 1, 0) for a in range(4)] +
              [xrow(a, 32, a ^ rank, 32, 64, 0, 31) for a in range(4)] +
              [io(T.TQ[quad(s), 4:8], [[1, 4]], -peer[s], 0) for s in range(4)]))
    i_t = R("g", [i_x], io(T.IT[:, :], [[1, 336]], 0, 0))
    i_b = R("g", [], io(T.NT[:, :], [[0, 4], [1, 84]], -4, 0),
            io(T.BI[:, 0:18], [[0, 6], [4, 3]], 0, 0), io(T.BI[:, 24:42], [[3, 6], [257, 3]], 0, 0))

    k3 = R("v", [k2, i_j, f_e],
           ts(T.TE[:, 3:515:4], J[:, :], c1(0), None, A.is_equal),
           ts(T.OR[:, :], J[:, 12:44:4], c1(4), 31.0, A.add, A.min),
           ts(T.DJ[:, :], J[:, 0:48], c1(3), None, A.subtract))
    k3a = R("a", [k2, i_j],
            act(CP[:, 7:8], c1(3), AF.Relu, bias=-86.0, scale=4.0),
            act(CP[:, 8:9], c1(3), AF.Relu, bias=12.0, scale=-8.0),
            act(CP[:, 9:10], c1(5), ID, bias=120.0),
            act(CP[:, 12:13], c1(2), ID, bias=c1(5), scale=-336.0),
            act(CP[:, 13:14], c1(2), ID, bias=c1(5), scale=4.0),
            act(CP[:, 14:15], c1(4), ID, bias=0.5),
            act(CP[:, 15:16], c1(1), ID, bias=16.0 / 1024, scale=1.0 / 1024),
            fill(T.W0[:, :], 96, -4.0), fill(T.WS[:, 0:88], 88, 1.0), fill(T.WS[:, 88:89], 1, 1.0 / 32))
    rr_s = R("a", [k3, q_a], picks("RR", 0, 128, "L0", 96, 128, T.OR[:, 0:8]))
    q_r1 = R("v", [l_r1, f_b], qz("R1", 0, 128, T.TB[:, :]))
    rr_c = R("v", [k3, q_a], pickc("RR", 0, 128, "L0", 96, 128, T.OR[:, 0:8]))
    q_e = [R("v", [k3], qz("E", 128 * b, 128 * b + 128, T.TE[:, 3 - b:515 - b])) for b in range(4)]
    wait("t", [rr_c, rr_s, q_r1])
    m_s = []
    for b in range(4):
        wait("t", [q_e[b]])
        mm(T.PD[:, 512 * b:512 * b + 128], "E", 128 * b, "RR", 0, 128, True, False)()
        m_s.append(R("t", [], mm(T.PD[:, 512 * b:512 * b + 128], "E", 128 * b, "R1", 0, 128, False, True)))
    q_r4 = R("v", [q_a, f_b, i_z], qz("R4", 0, 234, T.TA[:, :]), cp(T.OZ[:, :], T.BI[:, 48:56]))
    k4a = R("a", [k3a],
            act(T.C0[:, 88:89], c1(8), ID, bias=c1(7), scale=-1.0),
            act(CP[:, 11:12], c1(2), ID, bias=c1(9), scale=84.0),
            act(CP[:, 16:17], c1(12), ID, bias=-16.0),
            act(CP[:, 17:18], c1(14), ID, bias=c1(15)),
            *([act(T.TH0[:, 22 * s + 2:22 * s + 22], T.DJ[:, 2:22], ID, bias=20.0 * (peer[s] - rank) * EPS, scale=EPS) for s in range(4)] +
              [fill(T.TH0[:, 0:88:22], 4, HUGE), fill(T.TH0[:, 1:88:22], 4, HUGE)] +
              [fill(T.TX1[:, 336 * s:336 * s + 16], 16, 0.0) for s in range(4)]))
    c_s = R("a", m_s, *[act(T.S1[:, 80 * b:80 * b + 80], T.PD[:, 512 * b:512 * b + 80], AF.Copy) for b in range(4)])
    f_p = R("v", [], ms(T.PT[:, :], 0.0))
    z_c = R("v", [q_r4, f_b], pickc("LP2", 0, 16, "R4", 0, 32, T.OL[:, 4:5]))
    z_s = R("a", [q_r4, f_b], picks("LP2", 0, 16, "R4", 0, 32, T.OL[:, 4:5]))
    k7a = R("a", [f_p, k4a], fill(T.W0[:, 31:96:32], 3, c1(11)), *(
            [fill(T.PT[:, k:336:84], 4, HUGE) for k in range(4)] +
            [act(T.THS[:, 48 * h:48 * h + 48], T.DJ[:, :], ID, bias=(0.5 - 32 * h) * EPS, scale=EPS) for h in range(2)]))
    q_r2 = R("v", [l_r2], qz("R2", 0, 320, T.TR[:, :]))
    k5 = R("v", [i_x, k3a], cp(ZB[:, 16:28], ZB[:, 0:12]), cp(ZB[:, 48:60], ZB[:, 32:44]), cp(T.OX[:, 6:7], c1(13)))
    k7 = R("v", [k5], tr(T.XT[:, :], ZB[:, 0:64]))
    k8 = R("v", [k7], cp(T.OX[:, 0:8:4], T.XT[:, 0:64:32]))

    ur_c = R("v", [ac, asc, q_r4], pickc("UR", 0, 128, "L0", 96, 194, T.OZ[:, 0:8]))
    ur_s = R("a", [ac, asc, q_r4], picks("UR", 0, 128, "L0", 96, 194, T.OZ[:, 0:8]))
    uo_c = R("v", [], pickc("UO", 0, 128, "L0", 96, 128, T.OU[:, 0:8]))
    wait("t", [ac, asc, q_r4])
    for s in range(3):
        mm(T.PB[:, 0:128], "R4", 106 - 32 * s, "L0", 22 * s, 128, s == 0, False)()
    m_c = R("t", [], mm(T.PB[:, 0:128], "R4", 10, "L0", 66, 128, False, True))
    m_r = R("t", [ur_c, ur_s], mm(T.PA[:, 0:128], "UR", 0, "L0", 66, 128, True, True))
    m_h = [R("t", [c_s], mm(T.PD[:, 512 * b:512 * b + 128], "E", 128 * b, "L0", 66, 128, True, True)) for b in range(4)]
    c_h = [R("a", [m_h[b]], act(DH[:, 4 * b:4 * b + 4], T.PD[:, 512 * b + 41:512 * b + 108:22], AF.Copy)) for b in range(4)]
    x1 = [R("a", c_h + [c_s],
            *[act(T.TX1[:, 336 * s + 16 + b:336 * s + 336:4], T.S1[:, 80 * b:80 * b + 80], ID,
                  bias=DH[:, 4 * b + s:4 * b + s + 1]) for s in ss for b in range(4)]) for ss in ((0, 1), (2, 3))]
    x = d0 = R("v", [m_r, m_c], ts(T.D0[:, :], T.PA[:, 40:128], T.PB[:, 106:107], None, A.subtract))
    x = R("v", [x, k4a], tt(T.C0[:, 0:88], T.D0[:, :], T.TH0[:, :], A.is_gt))
    x = R("v", [x, k3a], scan(T.SA[:, 0:89], T.WS[:, 0:89], T.C0[:, 0:89]))
    x = R("v", [x, i_o], ts(T.M0[:, :], T.IO[:, :, :], T.SA[:, 21:22], T.SA[:, 88:89], A.is_equal, A.is_le))
    x = R("v", [x], tr(T.MT0[:, :], T.M0[:, :]))
    x = R("v", [x, k7a], scan(T.SC0[:, :], T.MT0[:, :], T.W0[:, :]))
    x = R("v", [x, f_x], cp(ZB[:, G0:G0 + 3], T.SC0[:, 31:96:32]), cp(ZB[LO, G0 + 3:G0 + 6], T.SC0[HI, 31:96:32]),
          cp(ZB[HI, G0 + 3:G0 + 6], T.SC0[LO, 31:96:32]))
    o_l = R("v", [z_c, z_s], cp(T.OL[:, 0:3], T.SC0[:, 31:96:32]))
    q_x1a = R("v", [x1[0]], qz("X1", 0, 168, T.TX1[:, 0:672]))
    n_p = R("a", [o_l, k7a, i_t], ga(T.NP[:, 0:64], T.IT[:, :], T.OL[:, 0:4]), ga(T.NP[:, 64:128], T.PT[:, :], T.OL[:, 0:4]))
    x = R("v", [x], *[cp(ZB[quad(a ^ 1), G0 + 16:G0 + 22], ZB[quad(a), G0:G0 + 6]) for a in range(4)])
    q_x1b = R("v", [x1[1]], qz("X1", 168, 336, T.TX1[:, 672:1344]))
    o_0 = R("v", [x, k8], cp(T.O0[:, :], ZB[:, G0:G0 + 32].indirect(T.OX[:, 0:1])))
    p1c = R("v", [o_0, q_x1a, q_x1b], pickc("P1", 0, 208, "X1", 0, 336, T.O0[:, 0:13]))
    p1s = R("a", [o_0, q_x1a, q_x1b], picks("P1", 0, 208, "X1", 0, 336, T.O0[:, 0:13]))
    npt = R("v", [n_p], tr(T.NPT[:, :], T.NP[:, :]))
    th1 = R("v", [], *[tt(T.TH1[:, 48 * h:48 * h + 48], T.NP[:, 64:112], T.THS[:, 48 * h:48 * h + 48], A.add) for h in range(2)])
    uo_s = R("a", [], picks("UO", 0, 128, "L0", 96, 128, T.OU[:, 0:8]))

    wait("g", [o_0])
    deal([T.O0[:, 3 * s:3 * s + 3] for s in far], T.LL0[:, 3 * rank:3 * rank + 3], m_b, "l0")
    wait("g", [p1c])
    deal([u8("P1c", 48 * s, 48 * s + 48) for s in far], u8("LP1c", 48 * rank, 48 * rank + 48), m_a, "p1")
    wait("g", [p1s])
    deal([T.P1s[:, 48 * s:48 * s + 48] for s in far], T.LP1s[:, 48 * rank:48 * rank + 48], m_b, "p1")
    h_l0 = D("s", [o_0], (T.LL0[:, 3 * rank:3 * rank + 3], T.O0[:, 0:3]))
    h_p1 = D("s", [p1c, p1s], (u8("LP1c", 48 * rank, 48 * rank + 48), u8("P1c", 0, 48)),
             (T.LP1s[:, 48 * rank:48 * rank + 48], T.P1s[:, 0:48]))
    l0 = ("l0", NE_)
    p1 = ("p1", 2 * NE_)

    m_1 = R("t", [p1c, p1s, d0], mm(T.PA[:, 0:208], "UR", 0, "P1", 0, 208, True, True))
    zt = R("v", [m_1], *[tr(T.ZT[quad(s), :], T.PA[quad(s), 48 * s:48 * s + 64]) for s in range(4)])
    x = R("v", [zt], tr(T.RA[:, :], T.ZT[:, :]))
    msa = R("a", [zt], act(T.ML[:, 0:2], T.ZT[:, 0:64:32], AF.Copy))
    k9a = R("a", [i_b, i_x], act(T.AB[:, 16:32], T.BI[:, 0:16], ID, bias=c1(14)),
            act(T.AB[:, 0:16], T.BI[:, 24:40], ID, bias=c1(17), scale=1.0 / 64),
            act(T.TQ[:, 0:4], T.TQ[:, 4:8], ID, scale=EPS),
            fill(T.RS[:, :], 128, 1.0), fill(T.NR[:, 0:16], 16, -1.0), fill(T.KT[:, 0:16], 16, 0.0),
            fill(T.KT[:, 16:112], 96, 1.0), fill(T.KT[:, 112:208], 96, 1.0),
            *[fill(T.NT[:, k:336:84], 4, -1.0) for k in range(3)])
    x = R("v", [x, npt], *[ts(T.D1[:, 48 * h:48 * h + 48], T.RA[:, 0:48], T.ZT[:, 32 * h:32 * h + 1],
                              T.NPT[:, 64 + 32 * h:65 + 32 * h], A.subtract, A.add) for h in range(2)])
    x = R("v", [x, th1], tt(T.C1[:, :], T.D1[:, :], T.TH1[:, :], A.is_ge))
    rk = R("v", [x], *[red(T.ML[:, 2 + h:3 + h], T.C1[:, 48 * h:48 * h + 48]) for h in range(2)])
    wait("g", [rk, msa])
    bcast(T.ML[:, 0:4], [T.ML[:, 4 * s:4 * s + 4] for s in far], mask(eng), "ms", "locB")
    msg = ("ms", (N - 1) * NE_)
    x = R("v", [rk], *[ts(T.M1[:, :, 32 * h:32 * h + 32], T.IO[:, :, :], T.ML[:, 2 + h:3 + h], T.NPT[:, 32 * h:32 * h + 1],
                          A.is_equal, A.mult) for h in range(2)])
    x = R("v", [x], tr(T.MT1[:, :], T.M1[:, :, :]))
    k10a = R("a", [k9a], fill(T.RS[:, 0:128:32], 4, 0.0),
             *[act(T.TQ[quad(s), peer[s]:peer[s] + 1], J[quad(s), 0:1], ID, bias=HUGE, scale=0.0) for s in range(4)])
    x = R("v", [x], *[red(ZB[:, G1 + c:G1 + c + 1], T.MT1[:, 64 * c:64 * c + 64]) for c in range(3)])
    g1v = R("v", [x], cp(ZB[LO, G1 + 3:G1 + 6], ZB[HI, G1:G1 + 3]), cp(ZB[HI, G1 + 3:G1 + 6], ZB[LO, G1:G1 + 3]))
    g1a = R("a", [x], *[act(ZB[o, G1 + c:G1 + c + 3], ZB[i, G1:G1 + 3], ID, bias=CP[i, 16:17], scale=4.0)
                        for o, c, i in ((ALL, 8, ALL), (LO, 11, HI), (HI, 11, LO))])
    g2v = R("v", [g1v, g1a], *[cp(ZB[quad(a ^ 1), G1 + 16:G1 + 30], ZB[quad(a), G1:G1 + 14]) for a in (0, 1)])
    g2a = R("a", [g1v, g1a], *[act(ZB[quad(a ^ 1), G1 + 16:G1 + 30], ZB[quad(a), G1:G1 + 14], AF.Copy) for a in (2, 3)])
    o_v = R("v", [g2v, g2a], cp(T.OV[:, :], ZB[:, G1:G1 + 32].indirect(T.OX[:, 0:1])))
    o_e = R("v", [], cp(T.OE[:, :], ZB[:, G1 + 8:G1 + 32].indirect(T.OX[:, 0:1])))
    v2c = R("v", [o_v], pickc("V2", 0, 192, "X1", 0, 336, T.OV[:, 0:12]))
    v2s = R("a", [o_v], picks("V2", 0, 192, "X1", 0, 336, T.OV[:, 0:12]))
    e2c = R("v", [o_e, q_r2], pickc("E2", 0, 192, "R2", 0, 320, T.OE[:, 0:12]))
    e2s = R("a", [o_e, q_r2], picks("E2", 0, 192, "R2", 0, 320, T.OE[:, 0:12]))
    wait("g", [o_e])
    deal([T.OE[:, 3 * s:3 * s + 3] for s in far], T.LL1[:, 3 * rank:3 * rank + 3], m_b, "l1")
    h_l1 = D("s", [o_e], (T.LL1[:, 3 * rank:3 * rank + 3], T.OE[:, 0:3]))
    l1 = ("l1", NE_)
    q_w = R("v", [l_w], qz("W", 0, 128, T.TW[:, :]))
    pa1 = R("a", [l0, h_l0], ga(T.PA1[:, :], T.PT[:, :], T.LL0[:, 0:12]))
    wait("t", [v2c, v2s] + c_h)
    for b in range(4):
        mm(T.PD[:, 512 * b:512 * b + 192], "E", 128 * b, "V2", 0, 192, True, False)()
    m_e = [R("t", [e2c, e2s], mm(T.PD[:, 512 * b:512 * b + 192], "E", 128 * b, "E2", 0, 192, False, True)) for b in range(4)]
    m_a1 = R("t", [p1, h_p1, uo_c, uo_s, d0], mm(T.PB[:, 0:192], "UO", 0, "LP1", 0, 192, True, True))
    m_y0 = R("t", [q_w], mm(T.PY[:, 0:192], "W", 0, "LP1", 0, 192, True, True))
    cs = []
    for b in range(4):
        sides = [(T.TX2[:, 192 * s + b:192 * s + 192:4], T.PD[:, 512 * b + 48 * s:512 * b + 48 * s + 48],
                  DH[:, 4 * b + s:4 * b + s + 1]) for s in range(4)]
        if b % 2 == 0:
            cs.append(R("a", [m_e[b]], *[act(o, i, ID, bias=h) for o, i, h in sides]))
        else:
            cs.append(R("v", [m_e[b]] + c_h, *[ts(o, i, h, None, A.add) for o, i, h in sides]))
    q_x2 = R("v", cs, qz("X2", 0, 192, T.TX2[:, :]))

    wait("g", [q_x2])
    deal([u8("X2c", 48 * s, 48 * s + 48) for s in far], u8("LP2c", 16 + 48 * rank, 64 + 48 * rank), m_a, "p2c")
    deal([T.X2s[:, 48 * s:48 * s + 48] for s in far], T.LP2s[:, 16 + 48 * rank:64 + 48 * rank], m_b, "p2s")
    h_p2 = D("s", [q_x2], (u8("LP2c", 16 + 48 * rank, 64 + 48 * rank), u8("X2c", 0, 48)),
             (T.LP2s[:, 16 + 48 * rank:64 + 48 * rank], T.X2s[:, 0:48]))
    p2c = ("p2c", NE_)
    p2s = ("p2s", NE_)
    locB = ("locB", 7 * NE_)

    cl = R("a", [msg, rk, msa, k7], ga(T.CL[:, :], T.ML[:, :], T.OX[:, 6:7]))
    rm = R("v", [m_a1, pa1], tt(T.RM[:, :], T.PB[:, 0:192], T.PA1[:, :], A.subtract))
    c_y0 = R("a", [m_y0], act(T.Y[:, 0:192], T.PY[:, 0:192], AF.Copy))
    lim = R("a", [cl], act(T.LIM[:, 0:2], T.CL[:, 2:4], ID, bias=31.5, scale=-1.0))
    fs = [R("v", [cl, rm, k10a], *[ts(T.F[:, 192 * h + 48 * q:192 * h + 48 * q + 48], T.RM[:, 48 * q:48 * q + 48], T.CL[:, h:h + 1],
                                      T.TQ[:, q:q + 1], A.subtract, A.is_gt) for q in range(N)]) for h in range(2)]
    o_a = R("a", [fs[0]], lambda: S.activation(T.JK[:, :], T.F[:, 0:192], AF.Copy, accum_out=T.O2[:, 0:1]))
    o_b = R("v", [fs[1]], red(T.O2[:, 1:2], T.F[:, 192:384]))
    x = R("v", [o_a, o_b, lim], tt(T.FG[:, 0:2], T.O2[:, 0:2], T.LIM[:, 0:2], A.is_lt))
    n2 = R("a", [l1, h_l1], ga(T.NR[:, 16:208], T.IT[:, :], T.LL1[:, 0:12]))
    x = R("v", [x], *[ts(T.Z2[o, c:c + 32], ZB[i, Z0:Z0 + 32], T.FG[i, 0:1], T.FG[i, 1:2], A.add, A.add)
                      for o, c, i in ((ALL, 0, ALL), (LO, 32, HI), (HI, 32, LO))])
    x = R("v", [x], tr(T.KR[:, 0:64], T.Z2[:, :]), *[tr(T.KR[quad(a), 64:128], T.Z2[quad(a ^ 1), :]) for a in range(4)])
    n1 = R("a", [], ga(T.NM[:, 0:192], T.NT[:, :], T.LL0[:, 0:12]))
    x = cnt = R("v", [x], scan(T.SCN[:, :], T.RS[:, :], T.KR[:, :]))
    x = R("v", [x], tt(T.FA[:, :], T.SCN[:, :].indirect(T.OX[:, 4:5]), T.AB[:, 0:16], A.min))
    x = R("v", [x], tt(T.FB[:, :], T.FA[:, :], T.AB[:, 16:32], A.subtract))
    fl = R("v", [x], ts(T.FL[:, :], T.FB[:, :], 1024.0, None, A.mult))
    D("s", [c_y0, cnt], (T.y[:, 0:192], T.Y[:, 0:192]))

    mk = R("a", [fl], ga(T.MK[:, :], T.KT[:, :], T.FL[:, 0:12]))
    xfc = R("v", [fl, p2c, h_p2], pickc("XF", 0, 192, "LP2", 0, 208, T.FL[:, 0:12]))
    m_y1 = R("t", [p2c, p2s, h_p2], mm(T.PY[:, 512:704], "W", 0, "LP2", 16, 192, True, True))
    xfs = R("a", [fl, p2s, h_p2], picks("XF", 0, 192, "LP2", 0, 208, T.FL[:, 0:12]))
    c_y1 = R("v", [m_y1, mk], tt(T.Y[:, 192:384], T.PY[:, 512:704], T.MK[:, :], A.mult))
    n3 = R("v", [n2], cp(T.NM[:, 192:384], T.NR[:, :].indirect(T.FL[:, 0:12])))
    D("s", [xfc], (T.oc[:, :], u8("XFc", 0, 192)))
    D("s", [c_y1], (T.y[:, 192:384], T.Y[:, 192:384]))
    D("a", [xfs], *[(T.osc[4 * k:4 * k + 4, :], T.XFs[32 * k:32 * k + 4, :]) for k in range(4)])
    D("s", [n1, n3], (T.nm[:, :], T.NM[0:1, :]))

    wait("g", [locA, locB])
    for name in total:
        if max(known[q].get(name, 0) for q in known) < total[name]:
            wait("g", [(name, total[name])])
